import numpy as np
import ml_dtypes


def mxq(x, axis, fmt="e4m3"):
    dtype, down = {"e4m3": (ml_dtypes.float8_e4m3fn, 7), "e5m2": (ml_dtypes.float8_e5m2, 14)}[fmt]
    v = np.moveaxis(np.asarray(x, np.float32).astype(ml_dtypes.bfloat16).astype(np.float64), axis, -1)
    blocks = v.reshape(v.shape[:-1] + (-1, 32))
    amax = np.abs(blocks).max(-1, keepdims=True)
    byte = np.maximum(np.where(amax > 0, np.frexp(amax)[1] - 1 + 127, 0) - down, 1)
    scale = np.exp2(byte - 127.0)
    codes = (blocks / scale).astype(np.float32).astype(dtype).astype(np.float64)
    return np.moveaxis((codes * scale).reshape(v.shape), -1, axis)


WIDE = False


def mx_kscale(k):
    if not WIDE:
        return np.ones(k)
    levels = np.array([10, -10, 5, -5, 0])
    if k % 512:
        return np.exp2(np.random.permutation(np.resize(levels, k // 32))).repeat(32)
    a = np.empty((k // 512, 16))
    for p in range(k // 512):
        a[p, :8] = np.random.permutation(np.resize(levels, 8))
        for g in range(8):
            far = levels[np.abs(levels - a[p, g]) >= 10]
            a[p, g + 8] = far[np.random.randint(len(far))]
    return np.exp2(a.ravel()).repeat(32)


def f64(x):
    return np.asarray(x).astype(np.float64)


def striped(idx):
    return np.tile(idx.reshape(-1, 16).T, (8, 1)).astype(np.uint16)


def unstriped(offs):
    return offs[:16].T.reshape(-1).astype(np.int64)


def pack_weight(w):
    k, n = w.shape
    w = f64(np.asarray(w, np.float32).astype(ml_dtypes.bfloat16)).reshape(k // 32, 32, n)
    amax = np.abs(w).max(1)
    byte = np.clip(np.where(amax > 0, np.frexp(amax)[1] - 1 + 127 - 7, 1), 1, 254)
    scaled = (w * np.exp2(127.0 - byte)[:, None, :]).reshape(k, n).astype(np.float32)
    words = np.ascontiguousarray(scaled.reshape(k // 512, 128, 4, n).transpose(0, 1, 3, 2)).astype(ml_dtypes.float8_e4m3fn).view(np.uint8)
    return words, np.ascontiguousarray(byte.astype(np.uint8).reshape(k // 512, 16, n))


def unpack_weight(words, scales):
    g, p, n, _ = words.shape
    vals = np.ascontiguousarray(words).view(ml_dtypes.float8_e4m3fn).astype(np.float64) * np.repeat(np.exp2(scales.astype(np.float64) - 127.0), 8, axis=1)[..., None]
    return vals.transpose(0, 1, 3, 2).reshape(g * 512, n)


def silu(v):
    return v / (1.0 + np.exp(-np.maximum(v, -700.0)))

def planes(y):
    n, m = y.shape
    v = y.astype(np.float32).astype(ml_dtypes.bfloat16).astype(np.float64).reshape(n // 32, 32, m)
    top = np.abs(v).max(1)
    byte = np.clip(np.where(top > 0, np.frexp(top)[1] - 1 + 127 - 7, 1), 1, 254)
    codes = (v * np.exp2(127.0 - byte)[:, None, :]).reshape(n, m).astype(np.float32).astype(ml_dtypes.float8_e4m3fn).view(np.uint8)
    words = codes.reshape(n // 512, 128, 4, m).transpose(0, 1, 3, 2)
    return np.ascontiguousarray(words), np.ascontiguousarray(byte.astype(np.uint8).reshape(n // 512, 16, m))


K, T, H = 512, 512, 512


def setup_inputs():
    n = np.random.standard_normal
    s = mx_kscale(K)[:, None]
    u = mx_kscale(H)
    packed_xT = pack_weight(n((K, T)) * s)
    return {
        "x_words": packed_xT[0],
        "x_scales": packed_xT[1],
        "w1": (n((K, H)) / np.sqrt(2 * K) / s * u).astype(np.float32),
        "w2": (n((K, H)) / np.sqrt(2 * K) / s * u).astype(np.float32),
        "w3": (n((H, H)) / np.sqrt(H) / u[:, None]).astype(np.float32),
        "pos1": striped(np.random.permutation(T)),
        "pos2": striped(np.random.permutation(T)),
        "pos3": striped(np.random.permutation(T)),
        "pos4": striped(np.random.permutation(T)),
    }


def reference(x_words, x_scales, w1, w2, w3, pos1, pos2, pos3, pos4):
    xq = unpack_weight(x_words, x_scales)
    y = mxq(f64(w1), 0, "e4m3").T @ xq
    e = mxq(f64(w2), 0, "e4m3").T @ xq
    z = np.maximum(np.maximum(np.maximum(silu(y + e[:, unstriped(pos1)]), silu(y + e[:, unstriped(pos2)])), silu(y + e[:, unstriped(pos3)])), silu(y + e[:, unstriped(pos4)]))
    out_0 = mxq(f64(w3), 0, "e4m3").T @ mxq(z, 0, "e4m3")
    return (out_0,) + planes(out_0)

@@ -1,0 +1,286 @@
+from contextlib import ExitStack
+
+import concourse.mybir as mybir
+from concourse.masks import make_identity
+
+F32 = mybir.dt.float32
+BF16 = mybir.dt.bfloat16
+I32 = mybir.dt.int32
+U32 = mybir.dt.uint32
+U16 = mybir.dt.uint16
+U8 = mybir.dt.uint8
+FP8X4 = mybir.dt.float8_e4m3fn_x4
+SILU = mybir.ActivationFunctionType.Silu
+MAX = mybir.AluOpType.max
+
+P = 128
+T = 512
+H = 512
+D = 4
+WINDOW = 704
+FLOPS = 3 * 2 * 512 * 512 * 512
+LOADS = (('w', 2, 0, 1, 'SP'), ('x', 'SP'), ('w', 1, 0, 1, 'SP'), ('l', 1), ('w', 2, 1, 2, 'SP'), ('sc', 'S'), ('l', 3), ('l', 0), ('w', 2, 2, 3, 'SP'), ('w', 2, 3, 4, 'SP'), ('w', 1, 1, 2, 'SP'), ('w', 1, 3, 4, 'SP'), ('w', 1, 2, 3, 'SP'), ('l', 2))
+STEPS = (('c', 2, 0, 'V'), ('c', 2, 1, 'S'), ('c', 2, 2, 'S'), ('c', 2, 3, 'S'), ('c', 1, 0, 'V'), ('c', 1, 3, 'S'), ('p', 1, 0, 'S'), ('c', 1, 1, 'S'), ('h', 2, 0, 'SV'), ('L', 'w', 3, 0, 4, 'SP'), ('e', 0, 0, 4, 1, 2, 1), ('e', 0, 0, 4, 0, 1, 7), ('c', 1, 2, 'S'), ('r', 0, 0, 4, 1), ('c3', 1, 'S'), ('p', 2, 1, 'S'), ('p', 1, 1, 'S'), ('e', 1, 0, 4, 1, 2, 2), ('p', 2, 2, 'S'), ('e', 0, 0, 4, 2, 3, 0), ('e', 1, 0, 4, 0, 1, 1), ('p', 1, 2, 'S'), ('p', 2, 3, 'S'), ('e', 0, 0, 4, 3, 4, 3), ('e', 2, 0, 2, 2, 4, 6), ('c3', 0, 'S'), ('e', 1, 0, 4, 2, 3, 5), ('p', 1, 3, 'S'), ('e', 3, 0, 2, 0, 2, 0), ('e', 3, 0, 2, 2, 4, 7), ('e', 2, 0, 2, 0, 2, 4), ('e', 2, 2, 2, 2, 4, 2), ('e', 1, 0, 4, 3, 4, 0), ('r', 1, 0, 4, 1), ('e', 2, 2, 2, 0, 2, 4), ('c3', 3, 'S'), ('r', 1, 0, 4, 2), ('e', 3, 2, 1, 0, 4, 3), ('r', 1, 0, 4, 3), ('r', 0, 0, 4, 2), ('c3', 2, 'S'), ('q3',), ('r', 0, 0, 4, 3), ('e', 3, 3, 1, 0, 3, 0), ('m', 3, 2, 1), ('m', 2, 0, 2), ('m', 2, 2, 2), ('m', 3, 0, 2), ('r', 3, 3, 1, 1), ('e', 3, 3, 1, 3, 4, 4), ('t', 0, 2, 'S'), ('r', 3, 3, 1, 2), ('r', 3, 3, 1, 3), ('t', 2, 1, 'S'), ('o', 2, 1, 'S'), ('q', 2, 1, 'V'), ('t', 3, 1, 'S'), ('o', 0, 2, 'SS'), ('q', 0, 2, 'V'), ('f', 3))
+TAGS = {'raw3_0': 'slot4'}
+UB, MMB = 5, 3
+
+
+def tile_picked_wedgecv_silu_lo_kernel(
+    tc, x_words, x_scales, w1, w2, w3, pos1, pos2, pos3, pos4, out_0, out_1, out_2
+):
+    nc = tc.nc
+    with ExitStack() as ctx:
+        keep = ctx.enter_context(tc.tile_pool(name="keep", bufs=1))
+        work = ctx.enter_context(tc.tile_pool(name="work", bufs=1))
+        psum = ctx.enter_context(tc.psum_pool(name="psum", bufs=1))
+        eng = {"V": nc.vector, "S": nc.scalar, "G": nc.gpsimd, "SP": nc.sync}
+        tiles = {}
+        turns = []
+        banks = []
+
+        def bank(shape):
+            banks.append(0)
+            return psum.tile(shape, F32, name="acc", tag="mm%d" % (len(banks) % MMB), bufs=1)
+
+        def held(shape, dtype, name):
+            tiles[name] = work.tile(shape, dtype, name=name, tag=TAGS.get(name, name), bufs=1, align_bytes=64)
+            return tiles[name]
+
+        def copy(e, out, in_):
+            if e == "S":
+                nc.scalar.copy(out=out, in_=in_)
+            else:
+                eng[e].tensor_copy(out=out, in_=in_)
+
+        x_codes = held([P, T], U32, "x_codes")
+        x_plane = held([P, T], U8, "x_plane")
+        nc.gpsimd.memset(x_plane[:].bitcast(I32), 0)
+        wv = {k: w.rearrange("(p j) c -> p j c", j=4) for k, w in ((1, w1), (2, w2), (3, w3))}
+        lists = [keep.tile([P, T // 16], U16, name="list%d" % d) for d in range(D)]
+        pos = (pos1, pos2, pos3, pos4)
+        xs = x_scales[0].bitcast(I32)
+        raw = {}
+
+        def load(*ld):
+            if ld[0] == "x":
+                eng[ld[1]].dma_start(out=x_codes[:].bitcast(I32), in_=x_words[0].rearrange("p c r -> p (c r)").bitcast(I32))
+            elif ld[0] == "sc":
+                for q in range(4):
+                    eng[ld[1]].dma_start(out=x_plane[32 * q : 32 * q + 4, :].bitcast(I32), in_=xs[4 * q : 4 * q + 4, :])
+            elif ld[0] == "l":
+                nc.sync.dma_start(lists[ld[1]][:], pos[ld[1]])
+            else:
+                which, t0, t1, q = ld[1:]
+                r = held([P, 4, P * (t1 - t0)], F32, "raw%d_%d" % (which, t0))
+                eng[q].dma_start(out=r[:], in_=wv[which][:, :, P * t0 : P * t1])
+                for t in range(t0, t1):
+                    raw[which, t] = r[:, :, P * (t - t0) : P * (t - t0 + 1)]
+
+        for ld in LOADS:
+            load(*ld)
+        warm = held([P, 1], F32, "warm")
+        warm2 = held([P, 1], F32, "warm2")
+        nc.gpsimd.memset(warm[:], 0.0)
+        nc.scalar.activation(out=warm2[:], in_=warm[:], func=SILU)
+
+        ident = held([P, P], F32, "ident")
+        make_identity(nc, ident[:])
+        e_sb = [held([P, WINDOW], F32, "e%d" % t) for t in range(4)]
+        for t in range(4):
+            nc.gpsimd.memset(e_sb[t][:, T:WINDOW], 0.0)
+        zT = held([P, 4, 2, 256], BF16, "zT")
+        g3 = held([P, H * 4], BF16, "g3")
+        o_codes = held([P, T], U32, "o_codes")
+        o_plane = held([P, T], U8, "o_plane")
+        o0v = out_0.rearrange("(p t) v -> p t v", t=4)
+        o1v = out_1[0].rearrange("p c r -> p (c r)").bitcast(I32)
+        o2v = out_2[0].bitcast(I32)
+
+        def quant(g, n, name):
+            codes = held([P, n], U32, name + "_codes")
+            plane = held([P, n], U8, name + "_plane")
+            nc.vector.quantize_mx(out=codes[:].bitcast(FP8X4), scales=plane[:], in_=g)
+
+        def cast(which, t, e):
+            g = held([P, P * 4], BF16, "c%d_%d" % (which, t))
+            copy(
+                e,
+                g[:].rearrange("p (c i j) -> p c j i", i=4, j=4),
+                raw[which, t].rearrange("p j (c i) -> p c j i", i=4),
+            )
+
+        def cast3(a, e):
+            copy(
+                e,
+                g3[:].rearrange("p (t m j) -> p m j t", t=4, j=4)[:, 32 * a : 32 * (a + 1)],
+                raw[3, a].rearrange("p j (m t) -> p m j t", t=4),
+            )
+
+        def product(which, t, e):
+            name = "w%d_%d" % (which, t)
+            quant(tiles["c%d_%d" % (which, t)][:], P, name)
+            acc = bank([P, T])
+            nc.tensor.matmul_mx(
+                out=acc[:],
+                lhsT=tiles[name + "_codes"][:].bitcast(FP8X4),
+                lhsT_scale=tiles[name + "_plane"][:],
+                rhs=x_codes[:].bitcast(FP8X4),
+                rhs_scale=x_plane[:],
+                start=True,
+                stop=True,
+            )
+            copy(e, e_sb[t][:, 0:T] if which == 2 else held([P, T], F32, "y%d" % t)[:], acc[:])
+
+        def edge(t, b0, nb, d0, d1, slot):
+            n = P * nb
+            key = "%d_%d" % (t, b0)
+            if "s" + key not in tiles:
+                held([P, 2, D, n // 2], BF16, "s" + key)
+            s = tiles["s" + key]
+            k = len(turns)
+            turns.append(k)
+            g = work.tile([P, d1 - d0, n], F32, name="g%s_%d" % (key, d0), tag="slot%d" % slot, bufs=1, align_bytes=64)
+            for d in range(d0, d1):
+                nc.vector.tensor_copy(out=g[:, d - d0, :], in_=e_sb[t][:].indirect(lists[d][:, 8 * b0 : 8 * (b0 + nb)]))
+            u = psum.tile([P, d1 - d0, n], F32, name="u", tag="u%d" % (k % UB), bufs=1)
+            y = tiles["y%d" % t]
+            blocks = [(d, b) for d in range(d1 - d0) for b in range(nb)]
+            for d, b in blocks:
+                nc.tensor.matmul(
+                    u[:, d, P * b : P * (b + 1)], lhsT=y[:, P * (b0 + b) : P * (b0 + b + 1)], rhs=ident[:],
+                    is_transpose=True, start=((d, b) == blocks[0]), stop=False,
+                )
+            for d, b in blocks:
+                nc.tensor.matmul(
+                    u[:, d, P * b : P * (b + 1)], lhsT=g[:, d, P * b : P * (b + 1)], rhs=ident[:],
+                    is_transpose=True, start=False, stop=((d, b) == blocks[-1]),
+                )
+            nc.scalar.activation(
+                out=s[:, :, d0:d1, :].rearrange("p h d (q i) -> p h (d q) i", i=2),
+                in_=u[:].rearrange("p d (q h i) -> p h (d q) i", h=2, i=2),
+                func=SILU,
+            )
+
+        def into_zT(t, b0, nb, a, b):
+            nc.vector.tensor_tensor(
+                out=zT[:, b0 : b0 + nb, :, 64 * t : 64 * (t + 1)].rearrange("p b h c -> p h b c"),
+                in0=a.rearrange("p h (b c) -> p h b c", c=64),
+                in1=b.rearrange("p h (b c) -> p h b c", c=64),
+                op=MAX,
+            )
+
+        def largest(t, b0, nb):
+            key = "%d_%d" % (t, b0)
+            s = tiles["s" + key]
+            m = held([P, 2, 2, 64 * nb], BF16, "m" + key)
+            nc.vector.tensor_tensor(out=m[:], in0=s[:, :, 0:2, :], in1=s[:, :, 2:4, :], op=MAX)
+            into_zT(t, b0, nb, m[:, :, 0, :], m[:, :, 1, :])
+
+        def running(t, b0, nb, d):
+            key = "%d_%d" % (t, b0)
+            s = tiles["s" + key]
+            if d == 1:
+                m = held([P, 2, 2, 64 * nb], BF16, "m" + key)
+                nc.vector.tensor_tensor(out=m[:, 0], in0=s[:, :, 0, :], in1=s[:, :, 1, :], op=MAX)
+            elif d == 2:
+                m = tiles["m" + key]
+                nc.vector.tensor_tensor(out=m[:, 1], in0=m[:, 0], in1=s[:, :, 2, :], op=MAX)
+            else:
+                into_zT(t, b0, nb, tiles["m" + key][:, 1], s[:, :, 3, :])
+
+        def turn(b0, nb, e):
+            n = P * nb
+            zp = bank([P, nb, 2, P])
+            for b in range(nb):
+                for h in range(2):
+                    nc.tensor.transpose(zp[:, b, h, :], zT[:, b0 + b, h, :].bitcast(F32), ident[:])
+            zq = held([P, n * 4], BF16, "zq%d" % b0)
+            copy(e, zq[:].bitcast(F32).rearrange("p (b v h) -> p b v h", h=2, v=P), zp[:].rearrange("p b h v -> p b v h"))
+            quant(zq[:], n, "z%d" % b0)
+
+        def project(b0, nb, e):
+            n = P * nb
+            v0 = P * b0
+            o_sb = held([P, 4, n], F32, "o%d" % b0)
+            per = T // n
+            for t0 in range(0, 4, per):
+                acc = bank([P, per, n])
+                for t in range(t0, t0 + per):
+                    nc.tensor.matmul_mx(
+                        out=acc[:, t - t0, :],
+                        lhsT=tiles["w3_codes"][:, P * t : P * (t + 1)].bitcast(FP8X4),
+                        lhsT_scale=tiles["w3_plane"][:, P * t : P * (t + 1)],
+                        rhs=tiles["z%d_codes" % b0][:].bitcast(FP8X4),
+                        rhs_scale=tiles["z%d_plane" % b0][:],
+                        start=True,
+                        stop=True,
+                    )
+                copy(e[t0 // per], o_sb[:, t0 : t0 + per, :], acc[:])
+            nc.sync.dma_start(out=o0v[:, :, v0 : v0 + n], in_=o_sb[:])
+
+        def planes(b0, nb, e):
+            n = P * nb
+            v0 = P * b0
+            ob = held([P, n * 4], BF16, "ob%d" % b0)
+            copy(
+                e,
+                ob[:].rearrange("p (c i t) -> p c t i", i=4, t=4),
+                tiles["o%d" % b0][:].rearrange("p t (c i) -> p c t i", i=4),
+            )
+            nc.vector.quantize_mx(out=o_codes[:, v0 : v0 + n].bitcast(FP8X4), scales=o_plane[:, v0 : v0 + n], in_=ob[:])
+            nc.sync.dma_start(out=o1v[:, v0 : v0 + n], in_=o_codes[:, v0 : v0 + n].bitcast(I32))
+
+        def finish(b0):
+            v0 = P * b0
+            o_sb = held([P, 4, P], F32, "o%d" % b0)
+            ob = held([P, P * 4], BF16, "ob%d" % b0)
+            for t0 in (0, 2):
+                acc = bank([P, 2, P])
+                for t in (t0, t0 + 1):
+                    nc.tensor.matmul_mx(
+                        out=acc[:, t - t0, :],
+                        lhsT=tiles["w3_codes"][:, P * t : P * (t + 1)].bitcast(FP8X4),
+                        lhsT_scale=tiles["w3_plane"][:, P * t : P * (t + 1)],
+                        rhs=tiles["z%d_codes" % b0][:].bitcast(FP8X4),
+                        rhs_scale=tiles["z%d_plane" % b0][:],
+                        start=True,
+                        stop=True,
+                    )
+                nc.vector.tensor_copy(
+                    out=ob[:].rearrange("p (v t) -> p v t", t=4)[:, :, t0 : t0 + 2], in_=acc[:].rearrange("p t v -> p v t")
+                )
+                nc.scalar.copy(out=o_sb[:, t0 : t0 + 2, :], in_=acc[:])
+                (nc.scalar if t0 else nc.sync).dma_start(
+                    out=o0v[:, t0 : t0 + 2, v0 : v0 + P], in_=o_sb[:, t0 : t0 + 2, :]
+                )
+            nc.vector.quantize_mx(out=o_codes[:, v0 : v0 + P].bitcast(FP8X4), scales=o_plane[:, v0 : v0 + P], in_=ob[:])
+            nc.sync.dma_start(out=o1v[:, v0 : v0 + P], in_=o_codes[:, v0 : v0 + P].bitcast(I32))
+
+        def halves(which, t, e):
+            name = "w%d_%d" % (which, t)
+            quant(tiles["c%d_%d" % (which, t)][:], P, name)
+            dest = e_sb[t] if which == 2 else held([P, T], F32, "y%d" % t)
+            for a in range(2):
+                cols = slice(256 * a, 256 * (a + 1))
+                acc = bank([P, 256])
+                nc.tensor.matmul_mx(
+                    out=acc[:],
+                    lhsT=tiles[name + "_codes"][:].bitcast(FP8X4),
+                    lhsT_scale=tiles[name + "_plane"][:],
+                    rhs=x_codes[:, cols].bitcast(FP8X4),
+                    rhs_scale=x_plane[:, cols],
+                    start=True,
+                    stop=True,
+                )
+                copy(e[a], dest[:, cols], acc[:])
+
+        def quant3():
+            quant(g3[:], H, "w3")
+
+        do = {"c": cast, "c3": cast3, "p": product, "e": edge, "m": largest, "r": running, "t": turn, "o": project, "q": planes, "q3": quant3, "f": finish, "h": halves, "L": load}
+        for step in STEPS:
+            do[step[0]](*step[1:])
+        for q in range(4):
+            (nc.scalar if q % 2 else nc.sync).dma_start(
+                out=o2v[4 * q : 4 * q + 4, :], in_=o_plane[32 * q : 32 * q + 4, :].bitcast(I32)
+            )

@@ -19,10 +19,10 @@ H = 512
 D = 4
 WINDOW = 704
 FLOPS = 3 * 2 * 512 * 512 * 512
-LOADS = (('w', 2, 0, 1, 'SP'), ('x', 'SP'), ('w', 1, 0, 1, 'SP'), ('l', 1), ('w', 2, 1, 2, 'SP'), ('sc', 'S'), ('l', 3), ('l', 0), ('w', 2, 2, 3, 'SP'), ('w', 2, 3, 4, 'SP'), ('w', 1, 1, 2, 'SP'), ('w', 1, 3, 4, 'SP'), ('w', 1, 2, 3, 'SP'), ('l', 2))
-STEPS = (('c', 2, 0, 'V'), ('c', 2, 1, 'S'), ('c', 2, 2, 'S'), ('c', 2, 3, 'S'), ('c', 1, 0, 'V'), ('c', 1, 3, 'S'), ('p', 1, 0, 'S'), ('c', 1, 1, 'S'), ('h', 2, 0, 'SV'), ('L', 'w', 3, 0, 4, 'SP'), ('e', 0, 0, 4, 1, 2, 1), ('e', 0, 0, 4, 0, 1, 7), ('c', 1, 2, 'S'), ('r', 0, 0, 4, 1), ('c3', 1, 'S'), ('p', 2, 1, 'S'), ('p', 1, 1, 'S'), ('e', 1, 0, 4, 1, 2, 2), ('p', 2, 2, 'S'), ('e', 0, 0, 4, 2, 3, 0), ('e', 1, 0, 4, 0, 1, 1), ('p', 1, 2, 'S'), ('p', 2, 3, 'S'), ('e', 0, 0, 4, 3, 4, 3), ('e', 2, 0, 2, 2, 4, 6), ('c3', 0, 'S'), ('e', 1, 0, 4, 2, 3, 5), ('p', 1, 3, 'S'), ('e', 3, 0, 2, 0, 2, 0), ('e', 3, 0, 2, 2, 4, 7), ('e', 2, 0, 2, 0, 2, 4), ('e', 2, 2, 2, 2, 4, 2), ('e', 1, 0, 4, 3, 4, 0), ('r', 1, 0, 4, 1), ('e', 2, 2, 2, 0, 2, 4), ('c3', 3, 'S'), ('r', 1, 0, 4, 2), ('e', 3, 2, 1, 0, 4, 3), ('r', 1, 0, 4, 3), ('r', 0, 0, 4, 2), ('c3', 2, 'S'), ('q3',), ('r', 0, 0, 4, 3), ('e', 3, 3, 1, 0, 3, 0), ('m', 3, 2, 1), ('m', 2, 0, 2), ('m', 2, 2, 2), ('m', 3, 0, 2), ('r', 3, 3, 1, 1), ('e', 3, 3, 1, 3, 4, 4), ('t', 0, 2, 'S'), ('r', 3, 3, 1, 2), ('r', 3, 3, 1, 3), ('t', 2, 1, 'S'), ('o', 2, 1, 'S'), ('q', 2, 1, 'V'), ('t', 3, 1, 'S'), ('o', 0, 2, 'SS'), ('q', 0, 2, 'V'), ('f', 3))
-TAGS = {'raw3_0': 'slot4'}
-UB, MMB = 5, 3
+LOADS = (('w', 2, 0, 1, 'SP'), ('w', 1, 0, 1, 'SP'), ('sc', 'SP'), ('x', 'SP'), ('w', 1, 1, 2, 'SP'), ('w', 2, 1, 2, 'SP'), ('l', 1), ('l', 0), ('l', 2), ('w', 2, 2, 4, 'SP'), ('w', 1, 2, 4, 'SP'), ('l', 3))
+STEPS = (('c', 2, 3, 'S'), ('L', 'w', 3, 0, 1, 'SP'), ('c', 2, 2, 'S'), ('c', 2, 1, 'V'), ('c', 2, 0, 'S'), ('c', 1, 0, 'S'), ('c', 1, 3, 'S'), ('h', 2, 0, 'SV'), ('p', 1, 0, 'S'), ('e', 0, 0, 4, 1, 2, 1), ('c', 1, 2, 'S'), ('e', 0, 0, 4, 0, 1, 6), ('p', 2, 1, 'S'), ('c', 1, 1, 'V'), ('p', 2, 2, 'S'), ('p', 1, 1, 'S'), ('r', 0, 0, 4, 1), ('e', 0, 0, 4, 2, 3, 7), ('r', 0, 0, 4, 2), ('p', 1, 2, 'S'), ('e', 1, 0, 4, 0, 1, 0), ('e', 1, 0, 4, 1, 2, 4), ('L', 'w', 3, 3, 4, 'SP'), ('c3', 0, 'S'), ('e', 2, 0, 2, 2, 4, 1), ('p', 1, 3, 'S'), ('r', 1, 0, 4, 1), ('p', 2, 3, 'S'), ('L', 'w', 3, 2, 3, 'SP'), ('c3', 2, 'S'), ('e', 2, 0, 2, 0, 2, 2), ('m', 2, 0, 2), ('e', 1, 0, 4, 2, 3, 3), ('r', 1, 0, 4, 2), ('e', 0, 0, 4, 3, 4, 6), ('e', 3, 0, 2, 0, 2, 5), ('e', 3, 0, 2, 2, 4, 7), ('e', 1, 0, 4, 3, 4, 1), ('e', 3, 3, 1, 0, 3, 4), ('r', 0, 0, 4, 3), ('e', 2, 2, 2, 0, 2, 2), ('e', 2, 2, 2, 2, 4, 7), ('m', 3, 0, 2), ('c3', 3, 'S'), ('r', 1, 0, 4, 3), ('L', 'w', 3, 1, 2, 'SP'), ('e', 3, 2, 1, 0, 4, 6), ('c3', 1, 'S'), ('m', 3, 2, 1), ('q3',), ('t', 0, 2, 'S'), ('m', 2, 2, 2), ('t', 2, 1, 'V'), ('o', 0, 2, 'SS'), ('r', 3, 3, 1, 1), ('e', 3, 3, 1, 3, 4, 4), ('r', 3, 3, 1, 2), ('r', 3, 3, 1, 3), ('t', 3, 1, 'V'), ('o', 2, 1, 'SS'), ('o', 3, 1, 'S'), ('q', 2, 1, 'V'), ('q', 0, 2, 'V'), ('q', 3, 1, 'V'))
+TAGS = {'c1_0': 'y1', 'c2_2': 'free1', 'raw3_0': 'slot5', 'raw3_1': 'slot6', 'raw3_2': 'y1', 'raw3_3': 'e0', 'c2_1': 'slot3', 'c1_1': 'free3', 'c1_2': 'slot8'}
+UB, MMB = 4, 4
 
 
 def tile_picked_wedgecv_silu_lo_kernel(
@@ -105,15 +105,15 @@ def tile_picked_wedgecv_silu_lo_kernel(
             g = held([P, P * 4], BF16, "c%d_%d" % (which, t))
             copy(
                 e,
-                g[:].rearrange("p (c i j) -> p c j i", i=4, j=4),
-                raw[which, t].rearrange("p j (c i) -> p c j i", i=4),
+                g[:].rearrange("p (c j) -> p c j", j=4),
+                raw[which, t].rearrange("p j c -> p c j"),
             )
 
         def cast3(a, e):
             copy(
                 e,
-                g3[:].rearrange("p (t m j) -> p m j t", t=4, j=4)[:, 32 * a : 32 * (a + 1)],
-                raw[3, a].rearrange("p j (m t) -> p m j t", t=4),
+                g3[:].rearrange("p (t m j) -> p t m j", t=4, j=4)[:, :, 32 * a : 32 * (a + 1)],
+                raw[3, a].rearrange("p j (m t) -> p t m j", t=4),
             )
 
         def product(which, t, e):
@@ -202,7 +202,7 @@ def tile_picked_wedgecv_silu_lo_kernel(
             n = P * nb
             v0 = P * b0
             o_sb = held([P, 4, n], F32, "o%d" % b0)
-            per = T // n
+            per = 4 // len(e)
             for t0 in range(0, 4, per):
                 acc = bank([P, per, n])
                 for t in range(t0, t0 + per):
@@ -224,8 +224,8 @@ def tile_picked_wedgecv_silu_lo_kernel(
             ob = held([P, n * 4], BF16, "ob%d" % b0)
             copy(
                 e,
-                ob[:].rearrange("p (c i t) -> p c t i", i=4, t=4),
-                tiles["o%d" % b0][:].rearrange("p t (c i) -> p c t i", i=4),
+                ob[:].rearrange("p (v t) -> p v t", t=4),
+                tiles["o%d" % b0][:].rearrange("p t v -> p v t"),
             )
             nc.vector.quantize_mx(out=o_codes[:, v0 : v0 + n].bitcast(FP8X4), scales=o_plane[:, v0 : v0 + n], in_=ob[:])
             nc.sync.dma_start(out=o1v[:, v0 : v0 + n], in_=o_codes[:, v0 : v0 + n].bitcast(I32))

@@ -19,9 +19,9 @@ H = 512
 D = 4
 WINDOW = 704
 FLOPS = 3 * 2 * 512 * 512 * 512
-LOADS = (('w', 2, 0, 1, 'SP'), ('w', 1, 0, 1, 'SP'), ('sc', 'SP'), ('x', 'SP'), ('w', 1, 1, 2, 'SP'), ('w', 2, 1, 2, 'SP'), ('l', 1), ('l', 0), ('l', 2), ('w', 2, 2, 4, 'SP'), ('w', 1, 2, 4, 'SP'), ('l', 3))
-STEPS = (('c', 2, 3, 'S'), ('L', 'w', 3, 0, 1, 'SP'), ('c', 2, 2, 'S'), ('c', 2, 1, 'V'), ('c', 2, 0, 'S'), ('c', 1, 0, 'S'), ('c', 1, 3, 'S'), ('h', 2, 0, 'SV'), ('p', 1, 0, 'S'), ('e', 0, 0, 4, 1, 2, 1), ('c', 1, 2, 'S'), ('e', 0, 0, 4, 0, 1, 6), ('p', 2, 1, 'S'), ('c', 1, 1, 'V'), ('p', 2, 2, 'S'), ('p', 1, 1, 'S'), ('r', 0, 0, 4, 1), ('e', 0, 0, 4, 2, 3, 7), ('r', 0, 0, 4, 2), ('p', 1, 2, 'S'), ('e', 1, 0, 4, 0, 1, 0), ('e', 1, 0, 4, 1, 2, 4), ('L', 'w', 3, 3, 4, 'SP'), ('c3', 0, 'S'), ('e', 2, 0, 2, 2, 4, 1), ('p', 1, 3, 'S'), ('r', 1, 0, 4, 1), ('p', 2, 3, 'S'), ('L', 'w', 3, 2, 3, 'SP'), ('c3', 2, 'S'), ('e', 2, 0, 2, 0, 2, 2), ('m', 2, 0, 2), ('e', 1, 0, 4, 2, 3, 3), ('r', 1, 0, 4, 2), ('e', 0, 0, 4, 3, 4, 6), ('e', 3, 0, 2, 0, 2, 5), ('e', 3, 0, 2, 2, 4, 7), ('e', 1, 0, 4, 3, 4, 1), ('e', 3, 3, 1, 0, 3, 4), ('r', 0, 0, 4, 3), ('e', 2, 2, 2, 0, 2, 2), ('e', 2, 2, 2, 2, 4, 7), ('m', 3, 0, 2), ('c3', 3, 'S'), ('r', 1, 0, 4, 3), ('L', 'w', 3, 1, 2, 'SP'), ('e', 3, 2, 1, 0, 4, 6), ('c3', 1, 'S'), ('m', 3, 2, 1), ('q3',), ('t', 0, 2, 'S'), ('m', 2, 2, 2), ('t', 2, 1, 'V'), ('o', 0, 2, 'SS'), ('r', 3, 3, 1, 1), ('e', 3, 3, 1, 3, 4, 4), ('r', 3, 3, 1, 2), ('r', 3, 3, 1, 3), ('t', 3, 1, 'V'), ('o', 2, 1, 'SS'), ('o', 3, 1, 'S'), ('q', 2, 1, 'V'), ('q', 0, 2, 'V'), ('q', 3, 1, 'V'))
-TAGS = {'c1_0': 'y1', 'c2_2': 'free1', 'raw3_0': 'slot5', 'raw3_1': 'slot6', 'raw3_2': 'y1', 'raw3_3': 'e0', 'c2_1': 'slot3', 'c1_1': 'free3', 'c1_2': 'slot8'}
+LOADS = (("w", 2, 0, 1, "SP"), ("x", "SP"), ("sc", "SP"), ("w", 1, 0, 1, "SP"), ("w", 2, 1, 2, "SP"), ("w", 1, 1, 2, "SP"), ("l", 0), ("l", 1), ("w", 2, 2, 4, "SP"), ("l", 2), ("l", 3), ("w", 1, 2, 4, "SP"), ("w", 3, 0, 4, "SP"))
+STEPS = (("c", 2, 0, "V"), ("h", 2, 0, "SS"), ("c", 1, 0, "V"), ("p", 1, 0, "S"), ("c", 2, 1, "V"), ("c", 1, 1, "S"), ("c", 2, 2, "S"), ("c", 1, 2, "S"), ("c", 2, 3, "S"), ("c", 1, 3, "S"), ("p", 2, 1, "S"), ("e", 0, 0, 4, 0, 0), ("e", 0, 0, 4, 1, 1), ("e", 0, 0, 4, 2, 2), ("e", 0, 0, 4, 3, 3), ("p", 1, 1, "S"), ("p", 2, 2, "S"), ("p", 1, 2, "S"), ("p", 2, 3, "S"), ("e", 1, 0, 4, 0, 4), ("e", 1, 0, 4, 1, 5), ("p", 1, 3, "S"), ("e", 1, 0, 4, 2, 6), ("c3", 0, "S"), ("e", 1, 0, 4, 3, 0), ("e", 2, 0, 4, 0, 1), ("c3", 1, "S"), ("e", 2, 0, 4, 1, 2), ("e", 2, 0, 4, 2, 3), ("e", 2, 0, 4, 3, 4), ("c3", 2, "S"), ("e", 3, 0, 4, 0, 5), ("e", 3, 0, 4, 1, 6), ("e", 3, 0, 4, 2, 0), ("e", 3, 0, 4, 3, 1), ("c3", 3, "S"), ("r", 0, 0, 2, 1, 4), ("r", 0, 2, 2, 1, 4), ("r", 0, 0, 2, 2, 4), ("r", 0, 0, 1, 3, 4), ("r", 0, 1, 1, 3, 4), ("r", 0, 2, 2, 2, 4), ("r", 0, 2, 1, 3, 4), ("r", 0, 3, 1, 3, 4), ("q3", 0), ("q3", 1), ("q3", 2), ("q3", 3), ("t", 0, 1, "S"), ("t", 1, 1, "S"), ("t", 2, 1, "S"), ("t", 3, 1, "V"), ("o", 0, 1, "S"), ("o", 1, 1, "S"), ("o", 2, 1, "S"), ("o", 3, 1, "SV"), ("b", 0, 1, "V"), ("q", 0, 1), ("b", 1, 1, "V"), ("q", 1, 1), ("s", 0, 2, "SP"), ("b", 2, 1, "V"), ("q", 2, 1), ("b", 3, 1, "V"), ("q", 3, 1), ("s", 2, 2, "SP"))
+TAGS = {"c2_1": "slot0", "w1_1_codes": "slot0", "c2_2": "slot3", "c1_2": "slot4", "c2_3": "slot5", "c1_3": "slot6", "g3_0": "w1_3_plane", "g3_1": "y1", "g3_2": "slot2", "g3_3": "slot1", "w3_0_codes": "slot3", "w3_1_codes": "slot4", "w3_2_codes": "slot5"}
 UB, MMB = 4, 4
 
 
@@ -88,8 +88,10 @@ def tile_picked_wedgecv_silu_lo_kernel(
         e_sb = [held([P, WINDOW], F32, "e%d" % t) for t in range(4)]
         for t in range(4):
             nc.gpsimd.memset(e_sb[t][:, T:WINDOW], 0.0)
-        zT = held([P, 4, 2, 256], BF16, "zT")
-        g3 = held([P, H * 4], BF16, "g3")
+        zT = held([P, 4 * H], BF16, "zT")[:].rearrange("p (b h c) -> p b h c", b=4, h=2)
+        s = held([P, D * 4 * H], BF16, "s")[:].rearrange("p (d b h c) -> p d b h c", d=D, b=4, h=2)
+        m = held([P, 2 * 4 * H], BF16, "m")[:].rearrange("p (d b h c) -> p d b h c", d=2, b=4, h=2)
+        ob = held([P, T * 4], BF16, "ob")
         o_codes = held([P, T], U32, "o_codes")
         o_plane = held([P, T], U8, "o_plane")
         o0v = out_0.rearrange("(p t) v -> p t v", t=4)
@@ -110,11 +112,8 @@ def tile_picked_wedgecv_silu_lo_kernel(
             )
 
         def cast3(a, e):
-            copy(
-                e,
-                g3[:].rearrange("p (t m j) -> p t m j", t=4, j=4)[:, :, 32 * a : 32 * (a + 1)],
-                raw[3, a].rearrange("p j (m t) -> p t m j", t=4),
-            )
+            g = held([P, P * 4], BF16, "g3_%d" % a)
+            copy(e, g[:].rearrange("p (m j) -> p m j", j=4), tiles["raw3_0"][:].rearrange("p j (m t) -> p t m j", t=4)[:, a])
 
         def product(which, t, e):
             name = "w%d_%d" % (which, t)
@@ -131,62 +130,37 @@ def tile_picked_wedgecv_silu_lo_kernel(
             )
             copy(e, e_sb[t][:, 0:T] if which == 2 else held([P, T], F32, "y%d" % t)[:], acc[:])
 
-        def edge(t, b0, nb, d0, d1, slot):
+        def edge(t, b0, nb, d, slot):
             n = P * nb
-            key = "%d_%d" % (t, b0)
-            if "s" + key not in tiles:
-                held([P, 2, D, n // 2], BF16, "s" + key)
-            s = tiles["s" + key]
             k = len(turns)
             turns.append(k)
-            g = work.tile([P, d1 - d0, n], F32, name="g%s_%d" % (key, d0), tag="slot%d" % slot, bufs=1, align_bytes=64)
-            for d in range(d0, d1):
-                nc.vector.tensor_copy(out=g[:, d - d0, :], in_=e_sb[t][:].indirect(lists[d][:, 8 * b0 : 8 * (b0 + nb)]))
-            u = psum.tile([P, d1 - d0, n], F32, name="u", tag="u%d" % (k % UB), bufs=1)
+            g = work.tile([P, n], F32, name="g%d_%d_%d" % (t, b0, d), tag="slot%d" % slot, bufs=1, align_bytes=64)
+            nc.vector.tensor_copy(out=g[:], in_=e_sb[t][:].indirect(lists[d][:, 8 * b0 : 8 * (b0 + nb)]))
+            u = psum.tile([P, n], F32, name="u", tag="u%d" % (k % UB), bufs=1)
             y = tiles["y%d" % t]
-            blocks = [(d, b) for d in range(d1 - d0) for b in range(nb)]
-            for d, b in blocks:
+            for b in range(nb):
                 nc.tensor.matmul(
-                    u[:, d, P * b : P * (b + 1)], lhsT=y[:, P * (b0 + b) : P * (b0 + b + 1)], rhs=ident[:],
-                    is_transpose=True, start=((d, b) == blocks[0]), stop=False,
+                    u[:, P * b : P * (b + 1)], lhsT=y[:, P * (b0 + b) : P * (b0 + b + 1)], rhs=ident[:],
+                    is_transpose=True, start=(b == 0), stop=False,
                 )
-            for d, b in blocks:
+            for b in range(nb):
                 nc.tensor.matmul(
-                    u[:, d, P * b : P * (b + 1)], lhsT=g[:, d, P * b : P * (b + 1)], rhs=ident[:],
-                    is_transpose=True, start=False, stop=((d, b) == blocks[-1]),
+                    u[:, P * b : P * (b + 1)], lhsT=g[:, P * b : P * (b + 1)], rhs=ident[:],
+                    is_transpose=True, start=False, stop=(b == nb - 1),
                 )
             nc.scalar.activation(
-                out=s[:, :, d0:d1, :].rearrange("p h d (q i) -> p h (d q) i", i=2),
-                in_=u[:].rearrange("p d (q h i) -> p h (d q) i", h=2, i=2),
+                out=s[:, d, b0 : b0 + nb, :, 64 * t : 64 * (t + 1)].rearrange("p b h (q i) -> p h b q i", i=2),
+                in_=u[:].rearrange("p (b q h i) -> p h b q i", h=2, q=32, i=2),
                 func=SILU,
             )
 
-        def into_zT(t, b0, nb, a, b):
+        def running(t0, b0, nb, d, t1):
+            where = (slice(b0, b0 + nb), slice(0, 2), slice(64 * t0, 64 * t1))
+            first = s[:, 0] if d == 1 else m[:, d - 2]
+            dest = zT if d == 3 else m[:, d - 1]
             nc.vector.tensor_tensor(
-                out=zT[:, b0 : b0 + nb, :, 64 * t : 64 * (t + 1)].rearrange("p b h c -> p h b c"),
-                in0=a.rearrange("p h (b c) -> p h b c", c=64),
-                in1=b.rearrange("p h (b c) -> p h b c", c=64),
-                op=MAX,
+                out=dest[(slice(0, P),) + where], in0=first[(slice(0, P),) + where], in1=s[:, d][(slice(0, P),) + where], op=MAX
             )
-
-        def largest(t, b0, nb):
-            key = "%d_%d" % (t, b0)
-            s = tiles["s" + key]
-            m = held([P, 2, 2, 64 * nb], BF16, "m" + key)
-            nc.vector.tensor_tensor(out=m[:], in0=s[:, :, 0:2, :], in1=s[:, :, 2:4, :], op=MAX)
-            into_zT(t, b0, nb, m[:, :, 0, :], m[:, :, 1, :])
-
-        def running(t, b0, nb, d):
-            key = "%d_%d" % (t, b0)
-            s = tiles["s" + key]
-            if d == 1:
-                m = held([P, 2, 2, 64 * nb], BF16, "m" + key)
-                nc.vector.tensor_tensor(out=m[:, 0], in0=s[:, :, 0, :], in1=s[:, :, 1, :], op=MAX)
-            elif d == 2:
-                m = tiles["m" + key]
-                nc.vector.tensor_tensor(out=m[:, 1], in0=m[:, 0], in1=s[:, :, 2, :], op=MAX)
-            else:
-                into_zT(t, b0, nb, tiles["m" + key][:, 1], s[:, :, 3, :])
 
         def turn(b0, nb, e):
             n = P * nb
@@ -208,8 +182,8 @@ def tile_picked_wedgecv_silu_lo_kernel(
                 for t in range(t0, t0 + per):
                     nc.tensor.matmul_mx(
                         out=acc[:, t - t0, :],
-                        lhsT=tiles["w3_codes"][:, P * t : P * (t + 1)].bitcast(FP8X4),
-                        lhsT_scale=tiles["w3_plane"][:, P * t : P * (t + 1)],
+                        lhsT=tiles["w3_%d_codes" % t][:].bitcast(FP8X4),
+                        lhsT_scale=tiles["w3_%d_plane" % t][:],
                         rhs=tiles["z%d_codes" % b0][:].bitcast(FP8X4),
                         rhs_scale=tiles["z%d_plane" % b0][:],
                         start=True,
@@ -218,43 +192,23 @@ def tile_picked_wedgecv_silu_lo_kernel(
                 copy(e[t0 // per], o_sb[:, t0 : t0 + per, :], acc[:])
             nc.sync.dma_start(out=o0v[:, :, v0 : v0 + n], in_=o_sb[:])
 
-        def planes(b0, nb, e):
+        def rounded(b0, nb, e):
             n = P * nb
-            v0 = P * b0
-            ob = held([P, n * 4], BF16, "ob%d" % b0)
             copy(
                 e,
-                ob[:].rearrange("p (v t) -> p v t", t=4),
+                ob[:, 4 * P * b0 : 4 * P * (b0 + nb)].rearrange("p (v t) -> p v t", t=4),
                 tiles["o%d" % b0][:].rearrange("p t v -> p v t"),
             )
-            nc.vector.quantize_mx(out=o_codes[:, v0 : v0 + n].bitcast(FP8X4), scales=o_plane[:, v0 : v0 + n], in_=ob[:])
-            nc.sync.dma_start(out=o1v[:, v0 : v0 + n], in_=o_codes[:, v0 : v0 + n].bitcast(I32))
 
-        def finish(b0):
-            v0 = P * b0
-            o_sb = held([P, 4, P], F32, "o%d" % b0)
-            ob = held([P, P * 4], BF16, "ob%d" % b0)
-            for t0 in (0, 2):
-                acc = bank([P, 2, P])
-                for t in (t0, t0 + 1):
-                    nc.tensor.matmul_mx(
-                        out=acc[:, t - t0, :],
-                        lhsT=tiles["w3_codes"][:, P * t : P * (t + 1)].bitcast(FP8X4),
-                        lhsT_scale=tiles["w3_plane"][:, P * t : P * (t + 1)],
-                        rhs=tiles["z%d_codes" % b0][:].bitcast(FP8X4),
-                        rhs_scale=tiles["z%d_plane" % b0][:],
-                        start=True,
-                        stop=True,
-                    )
-                nc.vector.tensor_copy(
-                    out=ob[:].rearrange("p (v t) -> p v t", t=4)[:, :, t0 : t0 + 2], in_=acc[:].rearrange("p t v -> p v t")
-                )
-                nc.scalar.copy(out=o_sb[:, t0 : t0 + 2, :], in_=acc[:])
-                (nc.scalar if t0 else nc.sync).dma_start(
-                    out=o0v[:, t0 : t0 + 2, v0 : v0 + P], in_=o_sb[:, t0 : t0 + 2, :]
-                )
-            nc.vector.quantize_mx(out=o_codes[:, v0 : v0 + P].bitcast(FP8X4), scales=o_plane[:, v0 : v0 + P], in_=ob[:])
-            nc.sync.dma_start(out=o1v[:, v0 : v0 + P], in_=o_codes[:, v0 : v0 + P].bitcast(I32))
+        def planes(b0, nb):
+            cols = slice(P * b0, P * (b0 + nb))
+            nc.vector.quantize_mx(
+                out=o_codes[:, cols].bitcast(FP8X4), scales=o_plane[:, cols], in_=ob[:, 4 * P * b0 : 4 * P * (b0 + nb)]
+            )
+
+        def words(b0, nb, q):
+            cols = slice(P * b0, P * (b0 + nb))
+            eng[q].dma_start(out=o1v[:, cols], in_=o_codes[:, cols].bitcast(I32))
 
         def halves(which, t, e):
             name = "w%d_%d" % (which, t)
@@ -274,10 +228,10 @@ def tile_picked_wedgecv_silu_lo_kernel(
                 )
                 copy(e[a], dest[:, cols], acc[:])
 
-        def quant3():
-            quant(g3[:], H, "w3")
+        def quant3(a):
+            quant(tiles["g3_%d" % a][:], P, "w3_%d" % a)
 
-        do = {"c": cast, "c3": cast3, "p": product, "e": edge, "m": largest, "r": running, "t": turn, "o": project, "q": planes, "q3": quant3, "f": finish, "h": halves, "L": load}
+        do = {"c": cast, "c3": cast3, "p": product, "e": edge, "r": running, "t": turn, "o": project, "b": rounded, "q": planes, "s": words, "q3": quant3, "h": halves, "L": load}
         for step in STEPS:
             do[step[0]](*step[1:])
         for q in range(4):

@@ -12,6 +12,7 @@ U8 = mybir.dt.uint8
 FP8X4 = mybir.dt.float8_e4m3fn_x4
 SILU = mybir.ActivationFunctionType.Silu
 MAX = mybir.AluOpType.max
+ADD = mybir.AluOpType.add
 
 P = 128
 T = 512
@@ -19,10 +20,7 @@ H = 512
 D = 4
 WINDOW = 704
 FLOPS = 3 * 2 * 512 * 512 * 512
-LOADS = (("w", 2, 0, 1, "SP"), ("x", "SP"), ("sc", "SP"), ("w", 1, 0, 1, "SP"), ("w", 2, 1, 2, "SP"), ("w", 1, 1, 2, "SP"), ("l", 0), ("l", 1), ("w", 2, 2, 4, "SP"), ("l", 2), ("l", 3), ("w", 1, 2, 4, "SP"), ("w", 3, 0, 4, "SP"))
-STEPS = (("c", 2, 0, "V"), ("h", 2, 0, "SS"), ("c", 1, 0, "V"), ("p", 1, 0, "S"), ("c", 2, 1, "V"), ("c", 1, 1, "S"), ("c", 2, 2, "S"), ("c", 1, 2, "S"), ("c", 2, 3, "S"), ("c", 1, 3, "S"), ("p", 2, 1, "S"), ("e", 0, 0, 4, 0, 0), ("e", 0, 0, 4, 1, 1), ("e", 0, 0, 4, 2, 2), ("e", 0, 0, 4, 3, 3), ("p", 1, 1, "S"), ("p", 2, 2, "S"), ("p", 1, 2, "S"), ("p", 2, 3, "S"), ("e", 1, 0, 4, 0, 4), ("e", 1, 0, 4, 1, 5), ("p", 1, 3, "S"), ("e", 1, 0, 4, 2, 6), ("c3", 0, "S"), ("e", 1, 0, 4, 3, 0), ("e", 2, 0, 4, 0, 1), ("c3", 1, "S"), ("e", 2, 0, 4, 1, 2), ("e", 2, 0, 4, 2, 3), ("e", 2, 0, 4, 3, 4), ("c3", 2, "S"), ("e", 3, 0, 4, 0, 5), ("e", 3, 0, 4, 1, 6), ("e", 3, 0, 4, 2, 0), ("e", 3, 0, 4, 3, 1), ("c3", 3, "S"), ("r", 0, 0, 2, 1, 4), ("r", 0, 2, 2, 1, 4), ("r", 0, 0, 2, 2, 4), ("r", 0, 0, 1, 3, 4), ("r", 0, 1, 1, 3, 4), ("r", 0, 2, 2, 2, 4), ("r", 0, 2, 1, 3, 4), ("r", 0, 3, 1, 3, 4), ("q3", 0), ("q3", 1), ("q3", 2), ("q3", 3), ("t", 0, 1, "S"), ("t", 1, 1, "S"), ("t", 2, 1, "S"), ("t", 3, 1, "V"), ("o", 0, 1, "S"), ("o", 1, 1, "S"), ("o", 2, 1, "S"), ("o", 3, 1, "SV"), ("b", 0, 1, "V"), ("q", 0, 1), ("b", 1, 1, "V"), ("q", 1, 1), ("s", 0, 2, "SP"), ("b", 2, 1, "V"), ("q", 2, 1), ("b", 3, 1, "V"), ("q", 3, 1), ("s", 2, 2, "SP"))
-TAGS = {"c2_1": "slot0", "w1_1_codes": "slot0", "c2_2": "slot3", "c1_2": "slot4", "c2_3": "slot5", "c1_3": "slot6", "g3_0": "w1_3_plane", "g3_1": "y1", "g3_2": "slot2", "g3_3": "slot1", "w3_0_codes": "slot3", "w3_1_codes": "slot4", "w3_2_codes": "slot5"}
-UB, MMB = 4, 4
+U_BANKS, MM_BANKS = 4, 4
 
 
 def tile_picked_wedgecv_silu_lo_kernel(
@@ -33,190 +31,108 @@ def tile_picked_wedgecv_silu_lo_kernel(
         keep = ctx.enter_context(tc.tile_pool(name="keep", bufs=1))
         work = ctx.enter_context(tc.tile_pool(name="work", bufs=1))
         psum = ctx.enter_context(tc.psum_pool(name="psum", bufs=1))
-        eng = {"V": nc.vector, "S": nc.scalar, "G": nc.gpsimd, "SP": nc.sync}
         tiles = {}
-        turns = []
-        banks = []
 
-        def bank(shape):
-            banks.append(0)
-            return psum.tile(shape, F32, name="acc", tag="mm%d" % (len(banks) % MMB), bufs=1)
-
-        def held(shape, dtype, name):
-            tiles[name] = work.tile(shape, dtype, name=name, tag=TAGS.get(name, name), bufs=1, align_bytes=64)
+        def held(shape, dtype, name, tag=None):
+            tiles[name] = work.tile(shape, dtype, name=name, tag=tag or name, bufs=1, align_bytes=64)
             return tiles[name]
 
         def copy(e, out, in_):
             if e == "S":
                 nc.scalar.copy(out=out, in_=in_)
             else:
-                eng[e].tensor_copy(out=out, in_=in_)
+                nc.vector.tensor_copy(out=out, in_=in_)
 
         x_codes = held([P, T], U32, "x_codes")
         x_plane = held([P, T], U8, "x_plane")
-        nc.gpsimd.memset(x_plane[:].bitcast(I32), 0)
+        nc.vector.memset(x_plane[:].bitcast(I32), 0)
         wv = {k: w.rearrange("(p j) c -> p j c", j=4) for k, w in ((1, w1), (2, w2), (3, w3))}
         lists = [keep.tile([P, T // 16], U16, name="list%d" % d) for d in range(D)]
         pos = (pos1, pos2, pos3, pos4)
         xs = x_scales[0].bitcast(I32)
         raw = {}
 
-        def load(*ld):
-            if ld[0] == "x":
-                eng[ld[1]].dma_start(out=x_codes[:].bitcast(I32), in_=x_words[0].rearrange("p c r -> p (c r)").bitcast(I32))
-            elif ld[0] == "sc":
-                for q in range(4):
-                    eng[ld[1]].dma_start(out=x_plane[32 * q : 32 * q + 4, :].bitcast(I32), in_=xs[4 * q : 4 * q + 4, :])
-            elif ld[0] == "l":
-                nc.sync.dma_start(lists[ld[1]][:], pos[ld[1]])
-            else:
-                which, t0, t1, q = ld[1:]
-                r = held([P, 4, P * (t1 - t0)], F32, "raw%d_%d" % (which, t0))
-                eng[q].dma_start(out=r[:], in_=wv[which][:, :, P * t0 : P * t1])
-                for t in range(t0, t1):
-                    raw[which, t] = r[:, :, P * (t - t0) : P * (t - t0 + 1)]
+        def load_w(which, t0, t1):
+            r = held([P, 4, P * (t1 - t0)], F32, "raw%d_%d" % (which, t0))
+            nc.sync.dma_start(out=r[:], in_=wv[which][:, :, P * t0 : P * t1])
+            for t in range(t0, t1):
+                raw[which, t] = r[:, :, P * (t - t0) : P * (t - t0 + 1)]
 
-        for ld in LOADS:
-            load(*ld)
+        def load_x():
+            nc.sync.dma_start(out=x_codes[:].bitcast(I32), in_=x_words[0].rearrange("p c r -> p (c r)").bitcast(I32))
+
+        def load_scales(*queues):
+            for q in range(4):
+                queues[q * len(queues) // 4].dma_start(out=x_plane[32 * q : 32 * q + 4, :].bitcast(I32), in_=xs[4 * q : 4 * q + 4, :])
+
+        def load_list(d):
+            nc.sync.dma_start(lists[d][:], pos[d])
+
+        load_w(2, 0, 1)
+        load_x()
+        load_scales(nc.sync)
+        load_w(1, 0, 1)
+        load_w(2, 1, 2)
+        load_w(1, 1, 2)
+        load_list(0)
+        load_list(1)
+        load_w(2, 2, 4)
+        load_list(2)
+        load_list(3)
+        load_w(1, 2, 4)
+        load_w(3, 0, 4)
+
+        zero = held([P, 1], F32, "zero")
         warm = held([P, 1], F32, "warm")
-        warm2 = held([P, 1], F32, "warm2")
-        nc.gpsimd.memset(warm[:], 0.0)
-        nc.scalar.activation(out=warm2[:], in_=warm[:], func=SILU)
-
+        nc.vector.memset(zero[:], 0.0)
+        nc.scalar.activation(out=warm[:], in_=zero[:], func=SILU)
         ident = held([P, P], F32, "ident")
         make_identity(nc, ident[:])
         e_sb = [held([P, WINDOW], F32, "e%d" % t) for t in range(4)]
         for t in range(4):
             nc.gpsimd.memset(e_sb[t][:, T:WINDOW], 0.0)
-        zT = held([P, 4 * H], BF16, "zT")[:].rearrange("p (b h c) -> p b h c", b=4, h=2)
-        s = held([P, D * 4 * H], BF16, "s")[:].rearrange("p (d b h c) -> p d b h c", d=D, b=4, h=2)
-        m = held([P, 2 * 4 * H], BF16, "m")[:].rearrange("p (d b h c) -> p d b h c", d=2, b=4, h=2)
-        ob = held([P, T * 4], BF16, "ob")
+        y_sb = [held([P, T], F32, "y%d" % t) for t in range(4)]
+        s = [held([P, 4 * H], BF16, "s%d" % d)[:].rearrange("p (b h c) -> p b h c", b=4, h=2) for d in range(D)]
         o_codes = held([P, T], U32, "o_codes")
         o_plane = held([P, T], U8, "o_plane")
         o0v = out_0.rearrange("(p t) v -> p t v", t=4)
         o1v = out_1[0].rearrange("p c r -> p (c r)").bitcast(I32)
         o2v = out_2[0].bitcast(I32)
 
-        def quant(g, n, name):
-            codes = held([P, n], U32, name + "_codes")
+        products = []
+        top = {}
+        wide = {}
+        turns = []
+
+        def bank(shape, k):
+            return psum.tile(shape, F32, name="bank", tag="bank%d" % k, bufs=1)
+
+        def quant(g, n, name, tag=None):
+            codes = held([P, n], U32, name + "_codes", tag)
             plane = held([P, n], U8, name + "_plane")
             nc.vector.quantize_mx(out=codes[:].bitcast(FP8X4), scales=plane[:], in_=g)
 
-        def cast(which, t, e):
-            g = held([P, P * 4], BF16, "c%d_%d" % (which, t))
-            copy(
-                e,
-                g[:].rearrange("p (c j) -> p c j", j=4),
-                raw[which, t].rearrange("p j c -> p c j"),
-            )
+        def cast(which, t, e, slot=None):
+            g = held([P, P * 4], BF16, "c%d_%d" % (which, t), None if slot is None else "slot%d" % slot)
+            copy(e, g[:].rearrange("p (c i j) -> p c j i", i=4, j=4), raw[which, t].rearrange("p j (c i) -> p c j i", i=4))
 
         def cast3(a, e):
-            g = held([P, P * 4], BF16, "g3_%d" % a)
-            copy(e, g[:].rearrange("p (m j) -> p m j", j=4), tiles["raw3_0"][:].rearrange("p j (m t) -> p t m j", t=4)[:, a])
-
-        def product(which, t, e):
-            name = "w%d_%d" % (which, t)
-            quant(tiles["c%d_%d" % (which, t)][:], P, name)
-            acc = bank([P, T])
-            nc.tensor.matmul_mx(
-                out=acc[:],
-                lhsT=tiles[name + "_codes"][:].bitcast(FP8X4),
-                lhsT_scale=tiles[name + "_plane"][:],
-                rhs=x_codes[:].bitcast(FP8X4),
-                rhs_scale=x_plane[:],
-                start=True,
-                stop=True,
-            )
-            copy(e, e_sb[t][:, 0:T] if which == 2 else held([P, T], F32, "y%d" % t)[:], acc[:])
-
-        def edge(t, b0, nb, d, slot):
-            n = P * nb
-            k = len(turns)
-            turns.append(k)
-            g = work.tile([P, n], F32, name="g%d_%d_%d" % (t, b0, d), tag="slot%d" % slot, bufs=1, align_bytes=64)
-            nc.vector.tensor_copy(out=g[:], in_=e_sb[t][:].indirect(lists[d][:, 8 * b0 : 8 * (b0 + nb)]))
-            u = psum.tile([P, n], F32, name="u", tag="u%d" % (k % UB), bufs=1)
-            y = tiles["y%d" % t]
-            for b in range(nb):
-                nc.tensor.matmul(
-                    u[:, P * b : P * (b + 1)], lhsT=y[:, P * (b0 + b) : P * (b0 + b + 1)], rhs=ident[:],
-                    is_transpose=True, start=(b == 0), stop=False,
-                )
-            for b in range(nb):
-                nc.tensor.matmul(
-                    u[:, P * b : P * (b + 1)], lhsT=g[:, P * b : P * (b + 1)], rhs=ident[:],
-                    is_transpose=True, start=False, stop=(b == nb - 1),
-                )
-            nc.scalar.activation(
-                out=s[:, d, b0 : b0 + nb, :, 64 * t : 64 * (t + 1)].rearrange("p b h (q i) -> p h b q i", i=2),
-                in_=u[:].rearrange("p (b q h i) -> p h b q i", h=2, q=32, i=2),
-                func=SILU,
-            )
-
-        def running(t0, b0, nb, d, t1):
-            where = (slice(b0, b0 + nb), slice(0, 2), slice(64 * t0, 64 * t1))
-            first = s[:, 0] if d == 1 else m[:, d - 2]
-            dest = zT if d == 3 else m[:, d - 1]
-            nc.vector.tensor_tensor(
-                out=dest[(slice(0, P),) + where], in0=first[(slice(0, P),) + where], in1=s[:, d][(slice(0, P),) + where], op=MAX
-            )
-
-        def turn(b0, nb, e):
-            n = P * nb
-            zp = bank([P, nb, 2, P])
-            for b in range(nb):
-                for h in range(2):
-                    nc.tensor.transpose(zp[:, b, h, :], zT[:, b0 + b, h, :].bitcast(F32), ident[:])
-            zq = held([P, n * 4], BF16, "zq%d" % b0)
-            copy(e, zq[:].bitcast(F32).rearrange("p (b v h) -> p b v h", h=2, v=P), zp[:].rearrange("p b h v -> p b v h"))
-            quant(zq[:], n, "z%d" % b0)
-
-        def project(b0, nb, e):
-            n = P * nb
-            v0 = P * b0
-            o_sb = held([P, 4, n], F32, "o%d" % b0)
-            per = 4 // len(e)
-            for t0 in range(0, 4, per):
-                acc = bank([P, per, n])
-                for t in range(t0, t0 + per):
-                    nc.tensor.matmul_mx(
-                        out=acc[:, t - t0, :],
-                        lhsT=tiles["w3_%d_codes" % t][:].bitcast(FP8X4),
-                        lhsT_scale=tiles["w3_%d_plane" % t][:],
-                        rhs=tiles["z%d_codes" % b0][:].bitcast(FP8X4),
-                        rhs_scale=tiles["z%d_plane" % b0][:],
-                        start=True,
-                        stop=True,
-                    )
-                copy(e[t0 // per], o_sb[:, t0 : t0 + per, :], acc[:])
-            nc.sync.dma_start(out=o0v[:, :, v0 : v0 + n], in_=o_sb[:])
-
-        def rounded(b0, nb, e):
-            n = P * nb
+            pair, rows = a // 2, slice(64 * (a % 2), 64 * (a % 2 + 1))
             copy(
                 e,
-                ob[:, 4 * P * b0 : 4 * P * (b0 + nb)].rearrange("p (v t) -> p v t", t=4),
-                tiles["o%d" % b0][:].rearrange("p t v -> p v t"),
+                tiles["w3_dealt"][:].rearrange("p (t m j) -> p m j t", t=4, j=4)[:, rows, :, 2 * pair : 2 * pair + 2],
+                tiles["raw3_0"][:].rearrange("p j (m t) -> p m j t", t=4)[:, rows, :, 2 * pair : 2 * pair + 2],
             )
 
-        def planes(b0, nb):
-            cols = slice(P * b0, P * (b0 + nb))
-            nc.vector.quantize_mx(
-                out=o_codes[:, cols].bitcast(FP8X4), scales=o_plane[:, cols], in_=ob[:, 4 * P * b0 : 4 * P * (b0 + nb)]
-            )
-
-        def words(b0, nb, q):
-            cols = slice(P * b0, P * (b0 + nb))
-            eng[q].dma_start(out=o1v[:, cols], in_=o_codes[:, cols].bitcast(I32))
-
-        def halves(which, t, e):
+        def product(which, t, es, tag=None):
             name = "w%d_%d" % (which, t)
-            quant(tiles["c%d_%d" % (which, t)][:], P, name)
-            dest = e_sb[t] if which == 2 else held([P, T], F32, "y%d" % t)
-            for a in range(2):
-                cols = slice(256 * a, 256 * (a + 1))
-                acc = bank([P, 256])
+            quant(tiles["c%d_%d" % (which, t)][:], P, name, tag)
+            dest = (e_sb if which == 2 else y_sb)[t]
+            n = T // len(es)
+            for a, e in enumerate(es):
+                cols = slice(n * a, n * (a + 1))
+                acc = bank([P, n], U_BANKS + len(products) % MM_BANKS)
+                products.append(name)
                 nc.tensor.matmul_mx(
                     out=acc[:],
                     lhsT=tiles[name + "_codes"][:].bitcast(FP8X4),
@@ -226,14 +142,132 @@ def tile_picked_wedgecv_silu_lo_kernel(
                     start=True,
                     stop=True,
                 )
-                copy(e[a], dest[:, cols], acc[:])
+                copy(e, dest[:, cols], acc[:])
 
-        def quant3(a):
-            quant(tiles["g3_%d" % a][:], P, "w3_%d" % a)
+        def edge(t, d, b0, nb, slot, plain, width=4):
+            n = P * nb
+            g = held([P, n], F32, "g%d_%d_%d" % (t, d, b0), "slot%d" % slot)
+            picked = e_sb[t][:].indirect(lists[d][:, 8 * b0 : 8 * (b0 + nb)])
+            y = y_sb[t][:, P * b0 : P * (b0 + nb)]
+            if plain:
+                nc.vector.tensor_copy(out=g[:], in_=picked)
+                terms = [y, g]
+            else:
+                nc.vector.tensor_tensor(out=g[:], in0=picked, in1=y, op=ADD)
+                terms = [g]
+            for c0 in range(0, nb, width):
+                u = bank([P, P * width], len(turns) % U_BANKS)
+                turns.append(d)
+                for k, term in enumerate(terms):
+                    for b in range(width):
+                        nc.tensor.matmul(
+                            u[:, P * b : P * (b + 1)], lhsT=term[:, P * (c0 + b) : P * (c0 + b + 1)], rhs=ident[:], is_transpose=True,
+                            start=(k == 0 and b == 0), stop=(k == len(terms) - 1 and b == width - 1),
+                        )
+                nc.scalar.activation(
+                    out=s[d][:, b0 + c0 : b0 + c0 + width, :, 64 * t : 64 * (t + 1)].rearrange("p b h (q i) -> p h b q i", i=2),
+                    in_=u[:].rearrange("p (b q h i) -> p h b q i", h=2, q=32, i=2),
+                    func=SILU,
+                )
 
-        do = {"c": cast, "c3": cast3, "p": product, "e": edge, "r": running, "t": turn, "o": project, "b": rounded, "q": planes, "s": words, "q3": quant3, "h": halves, "L": load}
-        for step in STEPS:
-            do[step[0]](*step[1:])
+        def running(d, b0, nb, tag=None):
+            dest = held([P, nb * H], BF16, "m%d_%d" % (d, b0), tag)
+            for b in range(b0, b0 + nb):
+                top[d, b] = dest[:, H * (b - b0) : H * (b - b0 + 1)]
+            span = slice(b0, b0 + nb)
+            first = s[0][:, span].rearrange("p b h c -> p (b h c)") if d == 1 else wide[d - 1, b0, nb]
+            nc.vector.tensor_tensor(out=dest[:], in0=first, in1=s[d][:, span].rearrange("p b h c -> p (b h c)"), op=MAX)
+            for c0 in range(nb):
+                for cn in range(1, nb - c0 + 1):
+                    wide[d, b0 + c0, cn] = dest[:, H * c0 : H * (c0 + cn)]
+
+        def turn(b, e, k):
+            zp = bank([P, 2, P], k)
+            for h in range(2):
+                nc.tensor.transpose(zp[:, h, :], top[D - 1, b][:, 2 * P * h : 2 * P * (h + 1)].bitcast(F32), ident[:])
+            zq = held([P, P * 4], BF16, "zq%d" % b)
+            copy(e, zq[:].bitcast(F32).rearrange("p (v h) -> p v h", h=2), zp[:].rearrange("p h v -> p v h"))
+
+        def squeeze(b):
+            quant(tiles["zq%d" % b][:], P, "z%d" % b)
+
+        def project(b, es, ks, direct=False):
+            o_sb = held([P, 4, P], F32, "o%d" % b)
+            ob = held([P, 4 * P], BF16, "ob%d" % b)
+            per = 4 // len(es)
+            for a, e in enumerate(es):
+                acc = bank([P, per, P], ks[a])
+                for t in range(per * a, per * (a + 1)):
+                    nc.tensor.matmul_mx(
+                        out=acc[:, t - per * a, :],
+                        lhsT=tiles["w3_codes"][:, P * t : P * (t + 1)].bitcast(FP8X4),
+                        lhsT_scale=tiles["w3_plane"][:, P * t : P * (t + 1)],
+                        rhs=tiles["z%d_codes" % b][:].bitcast(FP8X4),
+                        rhs_scale=tiles["z%d_plane" % b][:],
+                        start=True,
+                        stop=True,
+                    )
+                if direct:
+                    copy("V", ob[:].rearrange("p (v t) -> p v t", t=4), acc[:].rearrange("p t v -> p v t"))
+                copy(e, o_sb[:, per * a : per * (a + 1), :], acc[:])
+            nc.sync.dma_start(out=o0v[:, :, P * b : P * (b + 1)], in_=o_sb[:])
+
+        def rounded(b, e):
+            copy(
+                e,
+                tiles["ob%d" % b][:].rearrange("p (v i t) -> p v t i", i=4, t=4),
+                tiles["o%d" % b][:].rearrange("p t (v i) -> p v t i", i=4),
+            )
+
+        def planes(b):
+            cols = slice(P * b, P * (b + 1))
+            nc.vector.quantize_mx(out=o_codes[:, cols].bitcast(FP8X4), scales=o_plane[:, cols], in_=tiles["ob%d" % b][:])
+
+        def words(b0, nb):
+            cols = slice(P * b0, P * (b0 + nb))
+            nc.sync.dma_start(out=o1v[:, cols], in_=o_codes[:, cols].bitcast(I32))
+
+        cast(2, 0, "V")
+        product(2, 0, "SS")
+        cast(1, 0, "V")
+        product(1, 0, "S")
+        cast(2, 1, "V", 0)
+        cast(1, 1, "S")
+        for k, (which, t) in enumerate(((2, 2), (1, 2), (2, 3), (1, 3))):
+            cast(which, t, "S", 3 + k)
+        product(2, 1, "S")
+        for k in range(4 * D):
+            t, d = divmod(k, D)
+            if k == 4:
+                product(1, 1, "S", "slot0")
+                product(2, 2, "S")
+                product(1, 2, "S")
+                product(2, 3, "S")
+            if k == 6:
+                product(1, 3, "S")
+            if k == 8:
+                held([P, 4 * H], BF16, "w3_dealt", "y1")
+            edge(t, d, 0, 4, k % 7, t < 2, 4)
+            if 8 <= k < 12:
+                cast3(k - 8, "S")
+        running(1, 0, 2)
+        running(1, 2, 2)
+        running(2, 0, 2)
+        running(2, 2, 2)
+        for b in range(4):
+            running(3, b, 1)
+        quant(tiles["w3_dealt"][:], H, "w3", "m2_0")
+        for b in range(4):
+            turn(b, "S", 4 + b)
+            squeeze(b)
+        for b in range(3):
+            project(b, "S", [b])
+        project(3, "SV", [3, 4])
+        for b in range(4):
+            rounded(b, "V")
+            planes(b)
+            if b % 2:
+                words(b - 1, 2)
         for q in range(4):
             (nc.scalar if q % 2 else nc.sync).dma_start(
                 out=o2v[4 * q : 4 * q + 4, :], in_=o_plane[32 * q : 32 * q + 4, :].bitcast(I32)

@@ -73,8 +73,8 @@ def tile_picked_wedgecv_silu_lo_kernel(
         load_scales(nc.sync)
         load_w(1, 0, 1)
         load_w(2, 1, 2)
-        load_w(1, 1, 2)
         load_list(0)
+        load_w(1, 1, 2)
         load_list(1)
         load_w(2, 2, 4)
         load_list(2)
@@ -116,11 +116,18 @@ def tile_picked_wedgecv_silu_lo_kernel(
             g = held([P, P * 4], BF16, "c%d_%d" % (which, t), None if slot is None else "slot%d" % slot)
             copy(e, g[:].rearrange("p (c i j) -> p c j i", i=4, j=4), raw[which, t].rearrange("p j (c i) -> p c j i", i=4))
 
+        def quant3(tag):
+            codes = held([P, H], U32, "w3_codes", tag)
+            plane = held([P, H], U8, "w3_plane")
+            for pair in range(2):
+                cols = slice(2 * P * pair, 2 * P * (pair + 1))
+                nc.vector.quantize_mx(out=codes[:, cols].bitcast(FP8X4), scales=plane[:, cols], in_=tiles["w3_dealt%d" % pair][:])
+
         def cast3(a, e):
             pair, rows = a // 2, slice(64 * (a % 2), 64 * (a % 2 + 1))
             copy(
                 e,
-                tiles["w3_dealt"][:].rearrange("p (t m j) -> p m j t", t=4, j=4)[:, rows, :, 2 * pair : 2 * pair + 2],
+                tiles["w3_dealt%d" % pair][:].rearrange("p (t m j) -> p m j t", t=2, j=4)[:, rows],
                 tiles["raw3_0"][:].rearrange("p j (m t) -> p m j t", t=4)[:, rows, :, 2 * pair : 2 * pair + 2],
             )
 
@@ -246,23 +253,25 @@ def tile_picked_wedgecv_silu_lo_kernel(
             if k == 6:
                 product(1, 3, "S")
             if k == 8:
-                held([P, 4 * H], BF16, "w3_dealt", "y1")
+                held([P, 2 * H], BF16, "w3_dealt0", "y1")
             edge(t, d, 0, 4, k % 7, t < 2, 4)
-            if 8 <= k < 12:
+            if 8 <= k < 10:
                 cast3(k - 8, "S")
+        held([P, 2 * H], BF16, "w3_dealt1", "slot1")
+        cast3(2, "S")
+        cast3(3, "S")
         running(1, 0, 2)
         running(1, 2, 2)
         running(2, 0, 2)
         running(2, 2, 2)
         for b in range(4):
             running(3, b, 1)
-        quant(tiles["w3_dealt"][:], H, "w3", "m2_0")
+        quant3("m2_0")
         for b in range(4):
             turn(b, "S", 4 + b)
             squeeze(b)
-        for b in range(3):
+        for b in range(4):
             project(b, "S", [b])
-        project(3, "SV", [3, 4])
         for b in range(4):
             rounded(b, "V")
             planes(b)

@@ -72,12 +72,12 @@ def tile_picked_wedgecv_silu_lo_kernel(
         load_x()
         load_scales(nc.sync)
         load_w(1, 0, 1)
-        load_w(2, 1, 2)
         load_list(0)
-        load_w(1, 1, 2)
+        load_w(2, 1, 2)
         load_list(1)
-        load_w(2, 2, 4)
+        load_w(1, 1, 2)
         load_list(2)
+        load_w(2, 2, 4)
         load_list(3)
         load_w(1, 2, 4)
         load_w(3, 0, 4)
@@ -101,6 +101,7 @@ def tile_picked_wedgecv_silu_lo_kernel(
 
         products = []
         top = {}
+        coded = {}
         wide = {}
         turns = []
 
@@ -112,9 +113,21 @@ def tile_picked_wedgecv_silu_lo_kernel(
             plane = held([P, n], U8, name + "_plane")
             nc.vector.quantize_mx(out=codes[:].bitcast(FP8X4), scales=plane[:], in_=g)
 
-        def cast(which, t, e, slot=None):
-            g = held([P, P * 4], BF16, "c%d_%d" % (which, t), None if slot is None else "slot%d" % slot)
-            copy(e, g[:].rearrange("p (c i j) -> p c j i", i=4, j=4), raw[which, t].rearrange("p j (c i) -> p c j i", i=4))
+        def cast(group, e, slot=None):
+            g = held([P, 4 * P * len(group)], BF16, "c%d_%d" % group[0], None if slot is None else "slot%d" % slot)
+            for n, key in enumerate(group):
+                copy(
+                    e,
+                    g[:, 4 * P * n : 4 * P * (n + 1)].rearrange("p (c i j) -> p c j i", i=4, j=4),
+                    raw[key].rearrange("p j (c i) -> p c j i", i=4),
+                )
+
+        def squeeze_w(group, tag=None):
+            name = "w%d_%d" % group[0]
+            quant(tiles["c%d_%d" % group[0]][:], P * len(group), name, tag)
+            for n, key in enumerate(group):
+                cols = slice(P * n, P * (n + 1))
+                coded[key] = (tiles[name + "_codes"][:, cols], tiles[name + "_plane"][:, cols])
 
         def quant3(tag):
             codes = held([P, H], U32, "w3_codes", tag)
@@ -131,19 +144,17 @@ def tile_picked_wedgecv_silu_lo_kernel(
                 tiles["raw3_0"][:].rearrange("p j (m t) -> p m j t", t=4)[:, rows, :, 2 * pair : 2 * pair + 2],
             )
 
-        def product(which, t, es, tag=None):
-            name = "w%d_%d" % (which, t)
-            quant(tiles["c%d_%d" % (which, t)][:], P, name, tag)
+        def product(which, t, es):
             dest = (e_sb if which == 2 else y_sb)[t]
             n = T // len(es)
             for a, e in enumerate(es):
                 cols = slice(n * a, n * (a + 1))
                 acc = bank([P, n], U_BANKS + len(products) % MM_BANKS)
-                products.append(name)
+                products.append(t)
                 nc.tensor.matmul_mx(
                     out=acc[:],
-                    lhsT=tiles[name + "_codes"][:].bitcast(FP8X4),
-                    lhsT_scale=tiles[name + "_plane"][:],
+                    lhsT=coded[which, t][0].bitcast(FP8X4),
+                    lhsT_scale=coded[which, t][1],
                     rhs=x_codes[:, cols].bitcast(FP8X4),
                     rhs_scale=x_plane[:, cols],
                     start=True,
@@ -216,8 +227,9 @@ def tile_picked_wedgecv_silu_lo_kernel(
                     )
                 if direct:
                     copy("V", ob[:].rearrange("p (v t) -> p v t", t=4), acc[:].rearrange("p t v -> p v t"))
-                copy(e, o_sb[:, per * a : per * (a + 1), :], acc[:])
-            nc.sync.dma_start(out=o0v[:, :, P * b : P * (b + 1)], in_=o_sb[:])
+                rows = slice(per * a, per * (a + 1))
+                copy(e, o_sb[:, rows, :], acc[:])
+                nc.sync.dma_start(out=o0v[:, rows, P * b : P * (b + 1)], in_=o_sb[:, rows, :])
 
         def rounded(b, e):
             copy(
@@ -234,23 +246,29 @@ def tile_picked_wedgecv_silu_lo_kernel(
             cols = slice(P * b0, P * (b0 + nb))
             nc.sync.dma_start(out=o1v[:, cols], in_=o_codes[:, cols].bitcast(I32))
 
-        cast(2, 0, "V")
-        product(2, 0, "SS")
-        cast(1, 0, "V")
-        product(1, 0, "S")
-        cast(2, 1, "V", 0)
-        cast(1, 1, "S")
-        for k, (which, t) in enumerate(((2, 2), (1, 2), (2, 3), (1, 3))):
-            cast(which, t, "S", 3 + k)
-        product(2, 1, "S")
+        for key, es in (((2, 0), "SS"), ((1, 0), "S")):
+            cast([key], "V", 7)
+            squeeze_w([key])
+            product(*key, es)
+        cast([(2, 1)], "S", 2)
+        later = ([(2, 2), (1, 2)], [(2, 3), (1, 3)])
         for k in range(4 * D):
             t, d = divmod(k, D)
+            if k == 1:
+                squeeze_w([(2, 1)])
+                product(2, 1, "S")
+                cast([(1, 1)], "S")
+                cast(later[0], "S", 5)
+                cast(later[1], "S", 6)
             if k == 4:
-                product(1, 1, "S", "slot0")
+                squeeze_w([(1, 1)], "slot0")
+                product(1, 1, "S")
+                squeeze_w(later[0])
                 product(2, 2, "S")
                 product(1, 2, "S")
-                product(2, 3, "S")
             if k == 6:
+                squeeze_w(later[1])
+                product(2, 3, "S")
                 product(1, 3, "S")
             if k == 8:
                 held([P, 2 * H], BF16, "w3_dealt0", "y1")
@@ -270,13 +288,14 @@ def tile_picked_wedgecv_silu_lo_kernel(
         for b in range(4):
             turn(b, "S", 4 + b)
             squeeze(b)
+        project(0, "SS", [0, 4])
+        for b in range(1, 4):
+            project(b, "S", [b], b == 3)
         for b in range(4):
-            project(b, "S", [b])
-        for b in range(4):
-            rounded(b, "V")
+            if b < 3:
+                rounded(b, "V")
             planes(b)
-            if b % 2:
-                words(b - 1, 2)
+        words(0, 4)
         for q in range(4):
             (nc.scalar if q % 2 else nc.sync).dma_start(
                 out=o2v[4 * q : 4 * q + 4, :], in_=o_plane[32 * q : 32 * q + 4, :].bitcast(I32)

@@ -290,12 +290,12 @@ def tile_picked_wedgecv_silu_lo_kernel(
             squeeze(b)
         project(0, "SS", [0, 4])
         for b in range(1, 4):
-            project(b, "S", [b], b == 3)
+            project(b, "S", [b])
         for b in range(4):
-            if b < 3:
-                rounded(b, "V")
+            rounded(b, "V")
             planes(b)
-        words(0, 4)
+            if b % 2:
+                words(b - 1, 2)
         for q in range(4):
             (nc.scalar if q % 2 else nc.sync).dma_start(
                 out=o2v[4 * q : 4 * q + 4, :], in_=o_plane[32 * q : 32 * q + 4, :].bitcast(I32)

@@ -209,7 +209,7 @@ def tile_picked_wedgecv_silu_lo_kernel(
         def squeeze(b):
             quant(tiles["zq%d" % b][:], P, "z%d" % b)
 
-        def project(b, es, ks, direct=False):
+        def project(b, es, ks, direct=False, parts=(slice(0, P),)):
             o_sb = held([P, 4, P], F32, "o%d" % b)
             ob = held([P, 4 * P], BF16, "ob%d" % b)
             per = 4 // len(es)
@@ -228,15 +228,17 @@ def tile_picked_wedgecv_silu_lo_kernel(
                 if direct:
                     copy("V", ob[:].rearrange("p (v t) -> p v t", t=4), acc[:].rearrange("p t v -> p v t"))
                 rows = slice(per * a, per * (a + 1))
-                copy(e, o_sb[:, rows, :], acc[:])
+                for cols in parts:
+                    copy(e, o_sb[:, rows, cols], acc[:, :, cols])
                 nc.sync.dma_start(out=o0v[:, rows, P * b : P * (b + 1)], in_=o_sb[:, rows, :])
 
-        def rounded(b, e):
-            copy(
-                e,
-                tiles["ob%d" % b][:].rearrange("p (v i t) -> p v t i", i=4, t=4),
-                tiles["o%d" % b][:].rearrange("p t (v i) -> p v t i", i=4),
-            )
+        def rounded(b, e, parts):
+            for cols in parts:
+                copy(
+                    e,
+                    tiles["ob%d" % b][:, 4 * cols.start : 4 * cols.stop].rearrange("p (v i t) -> p v t i", i=4, t=4),
+                    tiles["o%d" % b][:, :, cols].rearrange("p t (v i) -> p v t i", i=4),
+                )
 
         def planes(b):
             cols = slice(P * b, P * (b + 1))
@@ -288,14 +290,14 @@ def tile_picked_wedgecv_silu_lo_kernel(
         for b in range(4):
             turn(b, "S", 4 + b)
             squeeze(b)
+        whole, halves = (slice(0, P),), (slice(0, P // 2), slice(P // 2, P))
         project(0, "SS", [0, 4])
         for b in range(1, 4):
-            project(b, "S", [b])
+            project(b, "S", [b], False, halves if b == 3 else whole)
         for b in range(4):
-            rounded(b, "V")
+            rounded(b, "V", halves if b == 3 else whole)
             planes(b)
-            if b % 2:
-                words(b - 1, 2)
+        words(0, 4)
         for q in range(4):
             (nc.scalar if q % 2 else nc.sync).dma_start(
                 out=o2v[4 * q : 4 * q + 4, :], in_=o_plane[32 * q : 32 * q + 4, :].bitcast(I32)

@@ -21,6 +21,8 @@ D = 4
 WINDOW = 704
 FLOPS = 3 * 2 * 512 * 512 * 512
 U_BANKS, MM_BANKS = 4, 4
+SLOT = 4 * T
+SLOTS = 8
 
 
 def tile_picked_wedgecv_silu_lo_kernel(
@@ -30,11 +32,15 @@ def tile_picked_wedgecv_silu_lo_kernel(
     with ExitStack() as ctx:
         keep = ctx.enter_context(tc.tile_pool(name="keep", bufs=1))
         work = ctx.enter_context(tc.tile_pool(name="work", bufs=1))
+        ring = ctx.enter_context(tc.tile_pool(name="ring", bufs=1))
         psum = ctx.enter_context(tc.psum_pool(name="psum", bufs=1))
         tiles = {}
 
         def held(shape, dtype, name, tag=None):
-            tiles[name] = work.tile(shape, dtype, name=name, tag=tag or name, bufs=1, align_bytes=64)
+            if isinstance(tag, int):
+                tiles[name] = ring.tile(shape, dtype, name=name, tag=name, bufs=1, align_bytes=64, offset=tag)
+            else:
+                tiles[name] = work.tile(shape, dtype, name=name, tag=tag or name, bufs=1, align_bytes=64)
             return tiles[name]
 
         def copy(e, out, in_):
@@ -113,10 +119,13 @@ def tile_picked_wedgecv_silu_lo_kernel(
             plane = held([P, n], U8, name + "_plane")
             nc.vector.quantize_mx(out=codes[:].bitcast(FP8X4), scales=plane[:], in_=g)
 
-        def cast(group, e, slot=None):
-            g = held([P, 4 * P * len(group)], BF16, "c%d_%d" % group[0], None if slot is None else "slot%d" % slot)
+        def cast(group, e, slot=None, spare=0, part=(0, 1)):
+            if 0 in part:
+                held([P, 4 * P * len(group) + spare], BF16, "c%d_%d" % group[0], slot)
+            g = tiles["c%d_%d" % group[0]]
             for n, key in enumerate(group):
-                copy(
+                if n in part:
+                  copy(
                     e,
                     g[:, 4 * P * n : 4 * P * (n + 1)].rearrange("p (c i j) -> p c j i", i=4, j=4),
                     raw[key].rearrange("p j (c i) -> p c j i", i=4),
@@ -124,7 +133,7 @@ def tile_picked_wedgecv_silu_lo_kernel(
 
         def squeeze_w(group, tag=None):
             name = "w%d_%d" % group[0]
-            quant(tiles["c%d_%d" % group[0]][:], P * len(group), name, tag)
+            quant(tiles["c%d_%d" % group[0]][:, 0 : 4 * P * len(group)], P * len(group), name, tag)
             for n, key in enumerate(group):
                 cols = slice(P * n, P * (n + 1))
                 coded[key] = (tiles[name + "_codes"][:, cols], tiles[name + "_plane"][:, cols])
@@ -162,9 +171,9 @@ def tile_picked_wedgecv_silu_lo_kernel(
                 )
                 copy(e, dest[:, cols], acc[:])
 
-        def edge(t, d, b0, nb, slot, plain, width=4):
+        def edge(t, d, b0, nb, slot, plain, width=4, between=None):
             n = P * nb
-            g = held([P, n], F32, "g%d_%d_%d" % (t, d, b0), "slot%d" % slot)
+            g = held([P, n], F32, "g%d_%d_%d" % (t, d, b0), SLOT * slot)
             picked = e_sb[t][:].indirect(lists[d][:, 8 * b0 : 8 * (b0 + nb)])
             y = y_sb[t][:, P * b0 : P * (b0 + nb)]
             if plain:
@@ -173,6 +182,8 @@ def tile_picked_wedgecv_silu_lo_kernel(
             else:
                 nc.vector.tensor_tensor(out=g[:], in0=picked, in1=y, op=ADD)
                 terms = [g]
+            if between:
+                between()
             for c0 in range(0, nb, width):
                 u = bank([P, P * width], len(turns) % U_BANKS)
                 turns.append(d)
@@ -248,36 +259,31 @@ def tile_picked_wedgecv_silu_lo_kernel(
             cols = slice(P * b0, P * (b0 + nb))
             nc.sync.dma_start(out=o1v[:, cols], in_=o_codes[:, cols].bitcast(I32))
 
-        for key, es in (((2, 0), "SS"), ((1, 0), "S")):
-            cast([key], "V", 7)
-            squeeze_w([key])
+        def astride(t):
+            return SLOT * ((D * t + 2) % SLOTS) - SLOT // 2 + (SLOT if t == 0 else 0)
+
+        def prepare(t):
+            squeeze_w([(2, t), (1, t)], astride(t) if t < 3 else "w3_held")
+            product(2, t, "S")
+            product(1, t, "S")
+            if t < 3:
+                cast([(2, t + 1), (1, t + 1)], "S", astride(t), 2 * T)
+
+        for part, (key, es, tag) in enumerate((((2, 0), "SS", astride(0)), ((1, 0), "S", None))):
+            cast([key], "V", "first")
+            squeeze_w([key], tag)
             product(*key, es)
-        cast([(2, 1)], "S", 2)
-        later = ([(2, 2), (1, 2)], [(2, 3), (1, 3)])
+            cast([(2, 1), (1, 1)], "S", astride(0), 0, (part,))
         for k in range(4 * D):
             t, d = divmod(k, D)
-            if k == 1:
-                squeeze_w([(2, 1)])
-                product(2, 1, "S")
-                cast([(1, 1)], "S")
-                cast(later[0], "S", 5)
-                cast(later[1], "S", 6)
-            if k == 4:
-                squeeze_w([(1, 1)], "slot0")
-                product(1, 1, "S")
-                squeeze_w(later[0])
-                product(2, 2, "S")
-                product(1, 2, "S")
-            if k == 6:
-                squeeze_w(later[1])
-                product(2, 3, "S")
-                product(1, 3, "S")
-            if k == 8:
-                held([P, 2 * H], BF16, "w3_dealt0", "y1")
-            edge(t, d, 0, 4, k % 7, t < 2, 4)
-            if 8 <= k < 10:
-                cast3(k - 8, "S")
-        held([P, 2 * H], BF16, "w3_dealt1", "slot1")
+            if k in (5, 9):
+                prepare(t + 1)
+            if k == 12:
+                held([P, 2 * H], BF16, "w3_dealt0", "w3_held")
+            edge(t, d, 0, 4, k % SLOTS, k < 2, 4, (lambda: prepare(1)) if k == 1 else None)
+            if 12 <= k < 14:
+                cast3(k - 12, "S")
+        held([P, 2 * H], BF16, "w3_dealt1", SLOT * 7)
         cast3(2, "S")
         cast3(3, "S")
         running(1, 0, 2)

@@ -22,7 +22,7 @@ WINDOW = 704
 FLOPS = 3 * 2 * 512 * 512 * 512
 U_BANKS, MM_BANKS = 4, 4
 SLOT = 4 * T
-SLOTS = 8
+SLOTS = 16
 
 
 def tile_picked_wedgecv_silu_lo_kernel(
@@ -58,9 +58,13 @@ def tile_picked_wedgecv_silu_lo_kernel(
         xs = x_scales[0].bitcast(I32)
         raw = {}
 
-        def load_w(which, t0, t1):
-            r = held([P, 4, P * (t1 - t0)], F32, "raw%d_%d" % (which, t0))
-            nc.sync.dma_start(out=r[:], in_=wv[which][:, :, P * t0 : P * t1])
+        def load_w(which, t0, t1, over=None):
+            if over:
+                wide_tile = held([P, T * len(over)], F32, "raw%d_%d" % (which, t0), SLOT * over[0])
+                r = wide_tile[:, 0:T].rearrange("p (j c) -> p j c", j=4)
+            else:
+                r = held([P, 4, P * (t1 - t0)], F32, "raw%d_%d" % (which, t0))[:]
+            nc.sync.dma_start(out=r, in_=wv[which][:, :, P * t0 : P * t1])
             for t in range(t0, t1):
                 raw[which, t] = r[:, :, P * (t - t0) : P * (t - t0 + 1)]
 
@@ -81,11 +85,12 @@ def tile_picked_wedgecv_silu_lo_kernel(
         load_list(0)
         load_w(2, 1, 2)
         load_list(1)
-        load_w(1, 1, 2)
+        load_w(1, 1, 2, (2, 3))
         load_list(2)
         load_w(2, 2, 4)
         load_list(3)
-        load_w(1, 2, 4)
+        load_w(1, 2, 3, (5, 6, 7))
+        load_w(1, 3, 4, (9, 10, 11))
         load_w(3, 0, 4)
 
         zero = held([P, 1], F32, "zero")
@@ -259,33 +264,40 @@ def tile_picked_wedgecv_silu_lo_kernel(
             cols = slice(P * b0, P * (b0 + nb))
             nc.sync.dma_start(out=o1v[:, cols], in_=o_codes[:, cols].bitcast(I32))
 
-        def astride(t):
-            return SLOT * ((D * t + 2) % SLOTS) - SLOT // 2 + (SLOT if t == 0 else 0)
-
         def prepare(t):
-            squeeze_w([(2, t), (1, t)], astride(t) if t < 3 else "w3_held")
+            squeeze_w([(2, t), (1, t)], "stage%d" % t)
             product(2, t, "S")
             product(1, t, "S")
             if t < 3:
-                cast([(2, t + 1), (1, t + 1)], "S", astride(t), 2 * T)
+                cast([(2, t + 1), (1, t + 1)], "S", "stage%d" % t)
 
-        for part, (key, es, tag) in enumerate((((2, 0), "SS", astride(0)), ((1, 0), "S", None))):
+        for part, (key, es, tag) in enumerate((((2, 0), "SS", "stage0"), ((1, 0), "S", None))):
             cast([key], "V", "first")
             squeeze_w([key], tag)
             product(*key, es)
-            cast([(2, 1), (1, 1)], "S", astride(0), 0, (part,))
+            cast([(2, 1), (1, 1)], "S", "stage0", 0, (part,))
         for k in range(4 * D):
             t, d = divmod(k, D)
             if k in (5, 9):
                 prepare(t + 1)
+            if k == 10:
+                held([P, 2 * H], BF16, "w3_dealt0", "stage3")
+            edge(t, d, 0, 4, k % SLOTS, k < 8, 4, (lambda: prepare(1)) if k == 1 else None)
             if k == 12:
-                held([P, 2 * H], BF16, "w3_dealt0", "w3_held")
-            edge(t, d, 0, 4, k % SLOTS, k < 2, 4, (lambda: prepare(1)) if k == 1 else None)
-            if 12 <= k < 14:
-                cast3(k - 12, "S")
-        held([P, 2 * H], BF16, "w3_dealt1", SLOT * 7)
-        cast3(2, "S")
-        cast3(3, "S")
+                held([P, 2 * H], BF16, "w3_dealt1", SLOT * 11)
+            if 10 <= k < 14:
+                cast3(k - 10, "S")
+        idle = bank([P, T], 2)
+        for n in range(3):
+            nc.tensor.matmul_mx(
+                out=idle[:],
+                lhsT=x_codes[:, 0:P].bitcast(FP8X4),
+                lhsT_scale=x_plane[:, 0:P],
+                rhs=x_codes[:].bitcast(FP8X4),
+                rhs_scale=x_plane[:],
+                start=True,
+                stop=True,
+            )
         running(1, 0, 2)
         running(1, 2, 2)
         running(2, 0, 2)
@@ -303,7 +315,8 @@ def tile_picked_wedgecv_silu_lo_kernel(
         for b in range(4):
             rounded(b, "V", halves if b == 3 else whole)
             planes(b)
-        words(0, 4)
+            if b % 2:
+                words(b - 1, 2)
         for q in range(4):
             (nc.scalar if q % 2 else nc.sync).dma_start(
                 out=o2v[4 * q : 4 * q + 4, :], in_=o_plane[32 * q : 32 * q + 4, :].bitcast(I32)

@@ -287,17 +287,6 @@ def tile_picked_wedgecv_silu_lo_kernel(
                 held([P, 2 * H], BF16, "w3_dealt1", SLOT * 11)
             if 10 <= k < 14:
                 cast3(k - 10, "S")
-        idle = bank([P, T], 2)
-        for n in range(3):
-            nc.tensor.matmul_mx(
-                out=idle[:],
-                lhsT=x_codes[:, 0:P].bitcast(FP8X4),
-                lhsT_scale=x_plane[:, 0:P],
-                rhs=x_codes[:].bitcast(FP8X4),
-                rhs_scale=x_plane[:],
-                start=True,
-                stop=True,
-            )
         running(1, 0, 2)
         running(1, 2, 2)
         running(2, 0, 2)

@@ -11,6 +11,7 @@ U16 = mybir.dt.uint16
 U8 = mybir.dt.uint8
 FP8X4 = mybir.dt.float8_e4m3fn_x4
 SILU = mybir.ActivationFunctionType.Silu
+COPY = mybir.ActivationFunctionType.Copy
 MAX = mybir.AluOpType.max
 ADD = mybir.AluOpType.add
 
@@ -176,12 +177,19 @@ def tile_picked_wedgecv_silu_lo_kernel(
                 )
                 copy(e, dest[:, cols], acc[:])
 
+        def fetch(t, d, slot):
+            g = held([P, T], F32, "g%d_%d_0" % (t, d), SLOT * slot)
+            nc.scalar.activation(out=g[:], in_=e_sb[t][:].indirect(lists[d][:]), func=COPY)
+
         def edge(t, d, b0, nb, slot, plain, width=4, between=None):
             n = P * nb
-            g = held([P, n], F32, "g%d_%d_%d" % (t, d, b0), SLOT * slot)
+            fetched = "g%d_%d_%d" % (t, d, b0) in tiles
+            g = tiles["g%d_%d_%d" % (t, d, b0)] if fetched else held([P, n], F32, "g%d_%d_%d" % (t, d, b0), SLOT * slot)
             picked = e_sb[t][:].indirect(lists[d][:, 8 * b0 : 8 * (b0 + nb)])
             y = y_sb[t][:, P * b0 : P * (b0 + nb)]
-            if plain:
+            if fetched:
+                terms = [y, g]
+            elif plain:
                 nc.vector.tensor_copy(out=g[:], in_=picked)
                 terms = [y, g]
             else:
@@ -283,10 +291,14 @@ def tile_picked_wedgecv_silu_lo_kernel(
             if k == 10:
                 held([P, 2 * H], BF16, "w3_dealt0", "stage3")
             edge(t, d, 0, 4, k % SLOTS, k < 8, 4, (lambda: prepare(1)) if k == 1 else None)
-            if k == 12:
-                held([P, 2 * H], BF16, "w3_dealt1", SLOT * 11)
-            if 10 <= k < 14:
-                cast3(k - 10, "S")
+            if k == 9:
+                fetch(3, 0, 12)
+            if k == 10:
+                cast3(0, "S")
+        held([P, 2 * H], BF16, "w3_dealt1", SLOT * 15)
+        cast3(1, "S")
+        cast3(2, "S")
+        cast3(3, "S")
         running(1, 0, 2)
         running(1, 2, 2)
         running(2, 0, 2)

@@ -14,6 +14,7 @@ SILU = mybir.ActivationFunctionType.Silu
 COPY = mybir.ActivationFunctionType.Copy
 MAX = mybir.AluOpType.max
 ADD = mybir.AluOpType.add
+MULT = mybir.AluOpType.mult
 
 P = 128
 T = 512
@@ -47,6 +48,8 @@ def tile_picked_wedgecv_silu_lo_kernel(
         def copy(e, out, in_):
             if e == "S":
                 nc.scalar.copy(out=out, in_=in_)
+            elif e == "G":
+                nc.gpsimd.tensor_scalar(out=out, in0=in_, scalar1=1.0, scalar2=0.0, op0=MULT, op1=ADD)
             else:
                 nc.vector.tensor_copy(out=out, in_=in_)
 
@@ -90,7 +93,7 @@ def tile_picked_wedgecv_silu_lo_kernel(
         load_list(2)
         load_w(2, 2, 4)
         load_list(3)
-        load_w(1, 2, 3, (5, 6, 7))
+        load_w(1, 2, 3, (6, 7))
         load_w(1, 3, 4, (9, 10, 11))
         load_w(3, 0, 4)
 
@@ -129,12 +132,13 @@ def tile_picked_wedgecv_silu_lo_kernel(
             if 0 in part:
                 held([P, 4 * P * len(group) + spare], BF16, "c%d_%d" % group[0], slot)
             g = tiles["c%d_%d" % group[0]]
+            order = "p c i j" if e == "G" else "p c j i"
             for n, key in enumerate(group):
                 if n in part:
                   copy(
                     e,
-                    g[:, 4 * P * n : 4 * P * (n + 1)].rearrange("p (c i j) -> p c j i", i=4, j=4),
-                    raw[key].rearrange("p j (c i) -> p c j i", i=4),
+                    g[:, 4 * P * n : 4 * P * (n + 1)].rearrange("p (c i j) -> " + order, i=4, j=4),
+                    raw[key].rearrange("p j (c i) -> " + order, i=4),
                 )
 
         def squeeze_w(group, tag=None):
@@ -151,12 +155,12 @@ def tile_picked_wedgecv_silu_lo_kernel(
                 cols = slice(2 * P * pair, 2 * P * (pair + 1))
                 nc.vector.quantize_mx(out=codes[:, cols].bitcast(FP8X4), scales=plane[:, cols], in_=tiles["w3_dealt%d" % pair][:])
 
-        def cast3(a, e):
+        def cast3(a, e, order):
             pair, rows = a // 2, slice(64 * (a % 2), 64 * (a % 2 + 1))
             copy(
                 e,
-                tiles["w3_dealt%d" % pair][:].rearrange("p (t m j) -> p m j t", t=2, j=4)[:, rows],
-                tiles["raw3_0"][:].rearrange("p j (m t) -> p m j t", t=4)[:, rows, :, 2 * pair : 2 * pair + 2],
+                tiles["w3_dealt%d" % pair][:].rearrange("p (t m j) -> " + order, t=2, j=4)[:, rows],
+                tiles["raw3_0"][:].rearrange("p j (m t) -> p m j t", t=4)[:, rows, :, 2 * pair : 2 * pair + 2].rearrange("p m j t -> " + order),
             )
 
         def product(which, t, es):
@@ -181,7 +185,7 @@ def tile_picked_wedgecv_silu_lo_kernel(
             g = held([P, T], F32, "g%d_%d_0" % (t, d), SLOT * slot)
             nc.scalar.activation(out=g[:], in_=e_sb[t][:].indirect(lists[d][:]), func=COPY)
 
-        def edge(t, d, b0, nb, slot, plain, width=4, between=None):
+        def edge(t, d, b0, nb, slot, plain, width=4, between=None, after=None):
             n = P * nb
             fetched = "g%d_%d_%d" % (t, d, b0) in tiles
             g = tiles["g%d_%d_%d" % (t, d, b0)] if fetched else held([P, n], F32, "g%d_%d_%d" % (t, d, b0), SLOT * slot)
@@ -198,7 +202,7 @@ def tile_picked_wedgecv_silu_lo_kernel(
             if between:
                 between()
             for c0 in range(0, nb, width):
-                u = bank([P, P * width], len(turns) % U_BANKS)
+                u = bank([P, P * width], len(turns) % U_BANKS if after is None else after)
                 turns.append(d)
                 for k, term in enumerate(terms):
                     for b in range(width):
@@ -274,10 +278,10 @@ def tile_picked_wedgecv_silu_lo_kernel(
 
         def prepare(t):
             squeeze_w([(2, t), (1, t)], "stage%d" % t)
+            if t < 3:
+                cast([(2, t + 1), (1, t + 1)], "G", "stage0")
             product(2, t, "S")
             product(1, t, "S")
-            if t < 3:
-                cast([(2, t + 1), (1, t + 1)], "S", "stage%d" % t)
 
         for part, (key, es, tag) in enumerate((((2, 0), "SS", "stage0"), ((1, 0), "S", None))):
             cast([key], "V", "first")
@@ -286,19 +290,19 @@ def tile_picked_wedgecv_silu_lo_kernel(
             cast([(2, 1), (1, 1)], "S", "stage0", 0, (part,))
         for k in range(4 * D):
             t, d = divmod(k, D)
-            if k in (5, 9):
-                prepare(t + 1)
-            if k == 10:
-                held([P, 2 * H], BF16, "w3_dealt0", "stage3")
-            edge(t, d, 0, 4, k % SLOTS, k < 8, 4, (lambda: prepare(1)) if k == 1 else None)
             if k == 9:
-                fetch(3, 0, 12)
-            if k == 10:
-                cast3(0, "S")
+                prepare(t + 1)
+            after = U_BANKS + len(products) % MM_BANKS if k == 5 else None
+            edge(t, d, 0, 4, k % SLOTS, k <= 8, 4, (lambda: prepare(t + 1)) if k in (1, 5) else None, after)
+            if k in (1, 9):
+                fetch(t + 1, 0, D * (t + 1))
+            if k == 6:
+                held([P, 2 * H], BF16, "w3_dealt0", "raw2_2")
+                cast3(0, "G", "p m t j")
+                cast3(1, "G", "p m t j")
         held([P, 2 * H], BF16, "w3_dealt1", SLOT * 15)
-        cast3(1, "S")
-        cast3(2, "S")
-        cast3(3, "S")
+        cast3(2, "S", "p m j t")
+        cast3(3, "S", "p m j t")
         running(1, 0, 2)
         running(1, 2, 2)
         running(2, 0, 2)

@@ -24,7 +24,7 @@ WINDOW = 704
 FLOPS = 3 * 2 * 512 * 512 * 512
 U_BANKS, MM_BANKS = 4, 4
 SLOT = 4 * T
-SLOTS = 16
+STAGE = 9 * SLOT
 
 
 def tile_picked_wedgecv_silu_lo_kernel(
@@ -94,7 +94,7 @@ def tile_picked_wedgecv_silu_lo_kernel(
         load_w(2, 2, 4)
         load_list(3)
         load_w(1, 2, 3, (6, 7))
-        load_w(1, 3, 4, (9, 10, 11))
+        load_w(1, 3, 4)
         load_w(3, 0, 4)
 
         zero = held([P, 1], F32, "zero")
@@ -118,7 +118,7 @@ def tile_picked_wedgecv_silu_lo_kernel(
         top = {}
         coded = {}
         wide = {}
-        turns = []
+        terms = {}
 
         def bank(shape, k):
             return psum.tile(shape, F32, name="bank", tag="bank%d" % k, bufs=1)
@@ -181,40 +181,32 @@ def tile_picked_wedgecv_silu_lo_kernel(
                 )
                 copy(e, dest[:, cols], acc[:])
 
-        def fetch(t, d, slot):
-            g = held([P, T], F32, "g%d_%d_0" % (t, d), SLOT * slot)
-            nc.scalar.activation(out=g[:], in_=e_sb[t][:].indirect(lists[d][:]), func=COPY)
-
-        def edge(t, d, b0, nb, slot, plain, width=4, between=None, after=None):
-            n = P * nb
-            fetched = "g%d_%d_%d" % (t, d, b0) in tiles
-            g = tiles["g%d_%d_%d" % (t, d, b0)] if fetched else held([P, n], F32, "g%d_%d_%d" % (t, d, b0), SLOT * slot)
-            picked = e_sb[t][:].indirect(lists[d][:, 8 * b0 : 8 * (b0 + nb)])
-            y = y_sb[t][:, P * b0 : P * (b0 + nb)]
-            if fetched:
-                terms = [y, g]
-            elif plain:
+        def gather(k, how):
+            t, d = divmod(k, D)
+            g = held([P, T], F32, "g%d" % k, SLOT * k)
+            picked = e_sb[t][:].indirect(lists[d][:])
+            if how == "S":
+                nc.scalar.activation(out=g[:], in_=picked, func=COPY)
+            elif how == "plain":
                 nc.vector.tensor_copy(out=g[:], in_=picked)
-                terms = [y, g]
             else:
-                nc.vector.tensor_tensor(out=g[:], in0=picked, in1=y, op=ADD)
-                terms = [g]
-            if between:
-                between()
-            for c0 in range(0, nb, width):
-                u = bank([P, P * width], len(turns) % U_BANKS if after is None else after)
-                turns.append(d)
-                for k, term in enumerate(terms):
-                    for b in range(width):
-                        nc.tensor.matmul(
-                            u[:, P * b : P * (b + 1)], lhsT=term[:, P * (c0 + b) : P * (c0 + b + 1)], rhs=ident[:], is_transpose=True,
-                            start=(k == 0 and b == 0), stop=(k == len(terms) - 1 and b == width - 1),
-                        )
-                nc.scalar.activation(
-                    out=s[d][:, b0 + c0 : b0 + c0 + width, :, 64 * t : 64 * (t + 1)].rearrange("p b h (q i) -> p h b q i", i=2),
-                    in_=u[:].rearrange("p (b q h i) -> p h b q i", h=2, q=32, i=2),
-                    func=SILU,
-                )
+                nc.vector.tensor_tensor(out=g[:], in0=picked, in1=y_sb[t][:], op=ADD)
+            terms[k] = [g] if how == "add" else [y_sb[t], g]
+
+        def edge(k, after=None):
+            t, d = divmod(k, D)
+            u = bank([P, T], k % U_BANKS if after is None else after)
+            for n, term in enumerate(terms[k]):
+                for b in range(4):
+                    nc.tensor.matmul(
+                        u[:, P * b : P * (b + 1)], lhsT=term[:, P * b : P * (b + 1)], rhs=ident[:], is_transpose=True,
+                        start=(n == 0 and b == 0), stop=(n == len(terms[k]) - 1 and b == 3),
+                    )
+            nc.scalar.activation(
+                out=s[d][:, :, :, 64 * t : 64 * (t + 1)].rearrange("p b h (q i) -> p h b q i", i=2),
+                in_=u[:].rearrange("p (b q h i) -> p h b q i", h=2, q=32, i=2),
+                func=SILU,
+            )
 
         def running(d, b0, nb, tag=None):
             dest = held([P, nb * H], BF16, "m%d_%d" % (d, b0), tag)
@@ -276,33 +268,48 @@ def tile_picked_wedgecv_silu_lo_kernel(
             cols = slice(P * b0, P * (b0 + nb))
             nc.sync.dma_start(out=o1v[:, cols], in_=o_codes[:, cols].bitcast(I32))
 
-        def prepare(t):
-            squeeze_w([(2, t), (1, t)], "stage%d" % t)
+        def prepare(t, tag):
+            squeeze_w([(2, t), (1, t)], tag)
             if t < 3:
-                cast([(2, t + 1), (1, t + 1)], "G", "stage0")
+                cast([(2, t + 1), (1, t + 1)], "G", STAGE, 2 * 2 * T if t == 2 else 0)
             product(2, t, "S")
             product(1, t, "S")
+            return [U_BANKS + (len(products) - n) % MM_BANKS for n in (2, 1)]
 
-        for part, (key, es, tag) in enumerate((((2, 0), "SS", "stage0"), ((1, 0), "S", None))):
+        for part, (key, es, tag) in enumerate((((2, 0), "SS", STAGE), ((1, 0), "S", None))):
             cast([key], "V", "first")
             squeeze_w([key], tag)
             product(*key, es)
-            cast([(2, 1), (1, 1)], "S", "stage0", 0, (part,))
-        for k in range(4 * D):
-            t, d = divmod(k, D)
-            if k == 9:
-                prepare(t + 1)
-            after = U_BANKS + len(products) % MM_BANKS if k == 5 else None
-            edge(t, d, 0, 4, k % SLOTS, k <= 8, 4, (lambda: prepare(t + 1)) if k in (1, 5) else None, after)
-            if k in (1, 9):
-                fetch(t + 1, 0, D * (t + 1))
-            if k == 6:
-                held([P, 2 * H], BF16, "w3_dealt0", "raw2_2")
-                cast3(0, "G", "p m t j")
-                cast3(1, "G", "p m t j")
-        held([P, 2 * H], BF16, "w3_dealt1", SLOT * 15)
-        cast3(2, "S", "p m j t")
-        cast3(3, "S", "p m j t")
+            cast([(2, 1), (1, 1)], "S", STAGE, 0, (part,))
+        gather(0, "plain")
+        edge(0)
+        gather(1, "add")
+        prepare(1, "stage1")
+        edge(1)
+        gather(4, "S")
+        for k in (2, 3):
+            gather(k, "plain")
+            edge(k)
+        gather(5, "add")
+        behind = prepare(2, "stage2")
+        edge(4, behind[0])
+        edge(5, behind[1])
+        gather(6, "plain")
+        edge(6)
+        gather(7, "plain")
+        edge(7)
+        gather(8, "plain")
+        behind = prepare(3, SLOT * 5)
+        gather(12, "S")
+        edge(8, behind[0])
+        for k in range(9, 4 * D):
+            if k != 12:
+                gather(k, "add")
+            edge(k)
+        for pair in range(2):
+            held([P, 2 * H], BF16, "w3_dealt%d" % pair, SLOT * (15 - pair))
+            cast3(2 * pair, "S", "p m j t")
+            cast3(2 * pair + 1, "S", "p m j t")
         running(1, 0, 2)
         running(1, 2, 2)
         running(2, 0, 2)

@@ -64,8 +64,8 @@ def tile_picked_wedgecv_silu_lo_kernel(
 
         def load_w(which, t0, t1, over=None):
             if over:
-                wide_tile = held([P, T * len(over)], F32, "raw%d_%d" % (which, t0), SLOT * over[0])
-                r = wide_tile[:, 0:T].rearrange("p (j c) -> p j c", j=4)
+                wide_tile = held([P, T * max(len(over), t1 - t0)], F32, "raw%d_%d" % (which, t0), SLOT * over[0])
+                r = wide_tile[:, 0 : T * (t1 - t0)].rearrange("p (j c) -> p j c", j=4)
             else:
                 r = held([P, 4, P * (t1 - t0)], F32, "raw%d_%d" % (which, t0))[:]
             nc.sync.dma_start(out=r, in_=wv[which][:, :, P * t0 : P * t1])
@@ -91,10 +91,10 @@ def tile_picked_wedgecv_silu_lo_kernel(
         load_list(1)
         load_w(1, 1, 2, (2, 3))
         load_list(2)
-        load_w(2, 2, 4)
+        load_w(2, 2, 4, (4,))
         load_list(3)
-        load_w(1, 2, 3, (6, 7))
-        load_w(1, 3, 4)
+        load_w(1, 2, 3)
+        load_w(1, 3, 4, (6, 7))
         load_w(3, 0, 4)
 
         zero = held([P, 1], F32, "zero")
@@ -106,7 +106,7 @@ def tile_picked_wedgecv_silu_lo_kernel(
         e_sb = [held([P, WINDOW], F32, "e%d" % t) for t in range(4)]
         for t in range(4):
             nc.gpsimd.memset(e_sb[t][:, T:WINDOW], 0.0)
-        y_sb = [held([P, T], F32, "y%d" % t) for t in range(4)]
+        y_sb = {t: held([P, T], F32, "y%d" % t) for t in range(4)}
         s = [held([P, 4 * H], BF16, "s%d" % d)[:].rearrange("p (b h c) -> p b h c", b=4, h=2) for d in range(D)]
         o_codes = held([P, T], U32, "o_codes")
         o_plane = held([P, T], U8, "o_plane")
@@ -118,7 +118,9 @@ def tile_picked_wedgecv_silu_lo_kernel(
         top = {}
         coded = {}
         wide = {}
-        terms = {}
+        plain = {}
+        sums = {}
+        place = {}
 
         def bank(shape, k):
             return psum.tile(shape, F32, name="bank", tag="bank%d" % k, bufs=1)
@@ -128,22 +130,25 @@ def tile_picked_wedgecv_silu_lo_kernel(
             plane = held([P, n], U8, name + "_plane")
             nc.vector.quantize_mx(out=codes[:].bitcast(FP8X4), scales=plane[:], in_=g)
 
-        def cast(group, e, slot=None, spare=0, part=(0, 1)):
-            if 0 in part:
-                held([P, 4 * P * len(group) + spare], BF16, "c%d_%d" % group[0], slot)
+        def stage(group, tag):
+            held([P, 4 * P * len(group)], BF16, "c%d_%d" % group[0], tag)
+
+        def cast(group, e, keys):
             g = tiles["c%d_%d" % group[0]]
             order = "p c i j" if e == "G" else "p c j i"
-            for n, key in enumerate(group):
-                if n in part:
-                  copy(
+            for key in keys:
+                n = group.index(key)
+                copy(
                     e,
                     g[:, 4 * P * n : 4 * P * (n + 1)].rearrange("p (c i j) -> " + order, i=4, j=4),
                     raw[key].rearrange("p j (c i) -> " + order, i=4),
                 )
 
-        def squeeze_w(group, tag=None):
+        def squeeze_w(group, tag=None, staged=None):
             name = "w%d_%d" % group[0]
-            quant(tiles["c%d_%d" % group[0]][:, 0 : 4 * P * len(group)], P * len(group), name, tag)
+            staged = staged or group
+            first = 4 * P * staged.index(group[0])
+            quant(tiles["c%d_%d" % staged[0]][:, first : first + 4 * P * len(group)], P * len(group), name, tag)
             for n, key in enumerate(group):
                 cols = slice(P * n, P * (n + 1))
                 coded[key] = (tiles[name + "_codes"][:, cols], tiles[name + "_plane"][:, cols])
@@ -180,10 +185,11 @@ def tile_picked_wedgecv_silu_lo_kernel(
                     stop=True,
                 )
                 copy(e, dest[:, cols], acc[:])
+            return U_BANKS + (len(products) - 1) % MM_BANKS
 
         def gather(k, how):
             t, d = divmod(k, D)
-            g = held([P, T], F32, "g%d" % k, SLOT * k)
+            g = held([P, T], F32, "g%d" % k, SLOT * (16 if k == 5 else k))
             picked = e_sb[t][:].indirect(lists[d][:])
             if how == "S":
                 nc.scalar.activation(out=g[:], in_=picked, func=COPY)
@@ -191,17 +197,27 @@ def tile_picked_wedgecv_silu_lo_kernel(
                 nc.vector.tensor_copy(out=g[:], in_=picked)
             else:
                 nc.vector.tensor_tensor(out=g[:], in0=picked, in1=y_sb[t][:], op=ADD)
-            terms[k] = [g] if how == "add" else [y_sb[t], g]
+            plain[k] = how != "add"
+
+        def move(u, source, start, stop):
+            for b in range(4):
+                nc.tensor.matmul(
+                    u[:, P * b : P * (b + 1)], lhsT=source[:, P * b : P * (b + 1)], rhs=ident[:], is_transpose=True,
+                    start=(start and b == 0), stop=(stop and b == 3),
+                )
+
+        def begin(k, after=None):
+            place[k] = k % U_BANKS if after is None else after
+            sums[k] = bank([P, T], place[k])
+            move(sums[k], tiles["g%d" % k], True, not plain[k])
 
         def edge(k, after=None):
             t, d = divmod(k, D)
-            u = bank([P, T], k % U_BANKS if after is None else after)
-            for n, term in enumerate(terms[k]):
-                for b in range(4):
-                    nc.tensor.matmul(
-                        u[:, P * b : P * (b + 1)], lhsT=term[:, P * b : P * (b + 1)], rhs=ident[:], is_transpose=True,
-                        start=(n == 0 and b == 0), stop=(n == len(terms[k]) - 1 and b == 3),
-                    )
+            if k not in sums:
+                begin(k, after)
+            u = sums[k]
+            if plain[k]:
+                move(u, y_sb[t], False, True)
             nc.scalar.activation(
                 out=s[d][:, :, :, 64 * t : 64 * (t + 1)].rearrange("p b h (q i) -> p h b q i", i=2),
                 in_=u[:].rearrange("p (b q h i) -> p h b q i", h=2, q=32, i=2),
@@ -268,48 +284,48 @@ def tile_picked_wedgecv_silu_lo_kernel(
             cols = slice(P * b0, P * (b0 + nb))
             nc.sync.dma_start(out=o1v[:, cols], in_=o_codes[:, cols].bitcast(I32))
 
-        def prepare(t, tag):
-            squeeze_w([(2, t), (1, t)], tag)
-            if t < 3:
-                cast([(2, t + 1), (1, t + 1)], "G", STAGE, 2 * 2 * T if t == 2 else 0)
-            product(2, t, "S")
-            product(1, t, "S")
-            return [U_BANKS + (len(products) - n) % MM_BANKS for n in (2, 1)]
-
-        for part, (key, es, tag) in enumerate((((2, 0), "SS", STAGE), ((1, 0), "S", None))):
-            cast([key], "V", "first")
+        second = [(2, 1), (1, 1)]
+        rest = [(2, 2), (1, 2), (2, 3), (1, 3)]
+        for key, es, tag in (((2, 0), "SS", "second"), ((1, 0), "S", None)):
+            stage([key], "first")
+            cast([key], "V", [key])
             squeeze_w([key], tag)
             product(*key, es)
-            cast([(2, 1), (1, 1)], "S", STAGE, 0, (part,))
+            if tag:
+                stage(second, tag)
+            cast(second, "S", [(key[0], 1)])
         gather(0, "plain")
         edge(0)
-        gather(1, "add")
-        prepare(1, "stage1")
-        edge(1)
+        gather(1, "plain")
+        squeeze_w(second, "third")
+        stage(rest, "second")
+        cast(rest, "G", [(2, 3), (1, 2), (1, 3)])
+        cast(rest, "S", rest[:1])
+        for key in second:
+            product(*key, "S")
         gather(4, "S")
+        edge(1)
         for k in (2, 3):
             gather(k, "plain")
             edge(k)
-        gather(5, "add")
-        behind = prepare(2, "stage2")
-        edge(4, behind[0])
-        edge(5, behind[1])
-        gather(6, "plain")
-        edge(6)
-        gather(7, "plain")
-        edge(7)
-        gather(8, "plain")
-        behind = prepare(3, SLOT * 5)
+        gather(5, "plain")
+        squeeze_w(rest[:2], None, rest)
+        squeeze_w(rest[2:], None, rest)
+        banks = [product(*key, "S") for key in rest]
         gather(12, "S")
-        edge(8, behind[0])
-        for k in range(9, 4 * D):
+        for k in (4, 5):
+            edge(k, banks[k - 4])
+        for k in range(6, 4 * D):
             if k != 12:
                 gather(k, "add")
             edge(k)
-        for pair in range(2):
-            held([P, 2 * H], BF16, "w3_dealt%d" % pair, SLOT * (15 - pair))
-            cast3(2 * pair, "S", "p m j t")
-            cast3(2 * pair + 1, "S", "p m j t")
+            if k == 13:
+                held([P, 2 * H], BF16, "w3_dealt0", SLOT * 13)
+            if k in (13, 14):
+                cast3(k - 13, "S", "p m j t")
+        held([P, 2 * H], BF16, "w3_dealt1", SLOT * 15)
+        cast3(2, "S", "p m j t")
+        cast3(3, "S", "p m j t")
         running(1, 0, 2)
         running(1, 2, 2)
         running(2, 0, 2)

@@ -24,7 +24,7 @@ WINDOW = 704
 FLOPS = 3 * 2 * 512 * 512 * 512
 U_BANKS, MM_BANKS = 4, 4
 SLOT = 4 * T
-STAGE = 9 * SLOT
+STAGE = 17 * SLOT
 
 
 def tile_picked_wedgecv_silu_lo_kernel(
@@ -93,8 +93,7 @@ def tile_picked_wedgecv_silu_lo_kernel(
         load_list(2)
         load_w(2, 2, 4, (4,))
         load_list(3)
-        load_w(1, 2, 3)
-        load_w(1, 3, 4, (6, 7))
+        load_w(1, 2, 4, (6, 7))
         load_w(3, 0, 4)
 
         zero = held([P, 1], F32, "zero")
@@ -130,8 +129,8 @@ def tile_picked_wedgecv_silu_lo_kernel(
             plane = held([P, n], U8, name + "_plane")
             nc.vector.quantize_mx(out=codes[:].bitcast(FP8X4), scales=plane[:], in_=g)
 
-        def stage(group, tag):
-            held([P, 4 * P * len(group)], BF16, "c%d_%d" % group[0], tag)
+        def stage(group, tag, room=0):
+            held([P, 4 * P * max(len(group), room)], BF16, "c%d_%d" % group[0], tag)
 
         def cast(group, e, keys):
             g = tiles["c%d_%d" % group[0]]
@@ -144,11 +143,9 @@ def tile_picked_wedgecv_silu_lo_kernel(
                     raw[key].rearrange("p j (c i) -> " + order, i=4),
                 )
 
-        def squeeze_w(group, tag=None, staged=None):
+        def squeeze_w(group, tag=None):
             name = "w%d_%d" % group[0]
-            staged = staged or group
-            first = 4 * P * staged.index(group[0])
-            quant(tiles["c%d_%d" % staged[0]][:, first : first + 4 * P * len(group)], P * len(group), name, tag)
+            quant(tiles["c%d_%d" % group[0]][:, 0 : 4 * P * len(group)], P * len(group), name, tag)
             for n, key in enumerate(group):
                 cols = slice(P * n, P * (n + 1))
                 coded[key] = (tiles[name + "_codes"][:, cols], tiles[name + "_plane"][:, cols])
@@ -189,7 +186,7 @@ def tile_picked_wedgecv_silu_lo_kernel(
 
         def gather(k, how):
             t, d = divmod(k, D)
-            g = held([P, T], F32, "g%d" % k, SLOT * (16 if k == 5 else k))
+            g = held([P, T], F32, "g%d" % k, SLOT * {5: 16, 11: 13}.get(k, k))
             picked = e_sb[t][:].indirect(lists[d][:])
             if how == "S":
                 nc.scalar.activation(out=g[:], in_=picked, func=COPY)
@@ -207,7 +204,7 @@ def tile_picked_wedgecv_silu_lo_kernel(
                 )
 
         def begin(k, after=None):
-            place[k] = k % U_BANKS if after is None else after
+            place[k] = len(place) % U_BANKS if after is None else after
             sums[k] = bank([P, T], place[k])
             move(sums[k], tiles["g%d" % k], True, not plain[k])
 
@@ -284,46 +281,50 @@ def tile_picked_wedgecv_silu_lo_kernel(
             cols = slice(P * b0, P * (b0 + nb))
             nc.sync.dma_start(out=o1v[:, cols], in_=o_codes[:, cols].bitcast(I32))
 
-        second = [(2, 1), (1, 1)]
-        rest = [(2, 2), (1, 2), (2, 3), (1, 3)]
-        for key, es, tag in (((2, 0), "SS", "second"), ((1, 0), "S", None)):
+        second, third, fourth = [[(2, t), (1, t)] for t in (1, 2, 3)]
+        for key, es, tag in (((2, 0), "SS", STAGE), ((1, 0), "S", None)):
             stage([key], "first")
             cast([key], "V", [key])
             squeeze_w([key], tag)
             product(*key, es)
             if tag:
-                stage(second, tag)
+                stage(second, tag, 4)
             cast(second, "S", [(key[0], 1)])
         gather(0, "plain")
         edge(0)
         gather(1, "plain")
-        squeeze_w(second, "third")
-        stage(rest, "second")
-        cast(rest, "G", [(2, 3), (1, 2), (1, 3)])
-        cast(rest, "S", rest[:1])
+        squeeze_w(second)
+        stage(third, STAGE)
+        stage(fourth, STAGE + SLOT)
+        cast(fourth, "G", [(2, 3)])
+        cast(third, "G", [(1, 2)])
+        cast(fourth, "G", [(1, 3)])
+        cast(third, "S", [(2, 2)])
         for key in second:
             product(*key, "S")
         gather(4, "S")
         edge(1)
-        for k in (2, 3):
-            gather(k, "plain")
-            edge(k)
+        gather(2, "plain")
+        edge(2)
+        gather(3, "plain")
         gather(5, "plain")
-        squeeze_w(rest[:2], None, rest)
-        squeeze_w(rest[2:], None, rest)
-        banks = [product(*key, "S") for key in rest]
+        squeeze_w(third)
+        squeeze_w(fourth)
+        held([P, 2 * H], BF16, "w3_dealt0", STAGE)
+        cast3(0, "G", "p m t j")
+        cast3(1, "G", "p m t j")
+        banks = [product(*key, "S") for key in third + fourth]
         gather(12, "S")
-        for k in (4, 5):
-            edge(k, banks[k - 4])
-        for k in range(6, 4 * D):
-            if k != 12:
-                gather(k, "add")
+        for k in (3, 4, 5):
+            edge(k, banks[k - 3])
+        for k in (6, 7, 8):
+            gather(k, "plain" if k < 8 else "add")
             edge(k)
-            if k == 13:
-                held([P, 2 * H], BF16, "w3_dealt0", SLOT * 13)
-            if k in (13, 14):
-                cast3(k - 13, "S", "p m j t")
-        held([P, 2 * H], BF16, "w3_dealt1", SLOT * 15)
+        edge(12)
+        for k in (9, 13, 10, 14, 15, 11):
+            gather(k, "add")
+            edge(k)
+        held([P, 2 * H], BF16, "w3_dealt1", SLOT * 13)
         cast3(2, "S", "p m j t")
         cast3(3, "S", "p m j t")
         running(1, 0, 2)

@@ -184,14 +184,16 @@ def tile_picked_wedgecv_silu_lo_kernel(
                 copy(e, dest[:, cols], acc[:])
             return U_BANKS + (len(products) - 1) % MM_BANKS
 
-        def gather(k, how):
+        def gather(k, how, cols=slice(0, T)):
             t, d = divmod(k, D)
-            g = held([P, T], F32, "g%d" % k, SLOT * {5: 16, 11: 13}.get(k, k))
-            picked = e_sb[t][:].indirect(lists[d][:])
+            if "g%d" % k not in tiles:
+                held([P, T], F32, "g%d" % k, SLOT * {5: 16, 11: 16}.get(k, k))
+            g = tiles["g%d" % k]
+            picked = e_sb[t][:].indirect(lists[d][:, cols.start // 16 : cols.stop // 16])
             if how == "S":
-                nc.scalar.activation(out=g[:], in_=picked, func=COPY)
+                nc.scalar.activation(out=g[:, cols], in_=picked, func=COPY)
             elif how == "plain":
-                nc.vector.tensor_copy(out=g[:], in_=picked)
+                nc.vector.tensor_copy(out=g[:, cols], in_=picked)
             else:
                 nc.vector.tensor_tensor(out=g[:], in0=picked, in1=y_sb[t][:], op=ADD)
             plain[k] = how != "add"
@@ -307,6 +309,7 @@ def tile_picked_wedgecv_silu_lo_kernel(
         gather(2, "plain")
         edge(2)
         gather(3, "plain")
+        edge(3)
         gather(5, "plain")
         squeeze_w(third)
         squeeze_w(fourth)
@@ -315,16 +318,18 @@ def tile_picked_wedgecv_silu_lo_kernel(
         cast3(1, "G", "p m t j")
         banks = [product(*key, "S") for key in third + fourth]
         gather(12, "S")
-        for k in (3, 4, 5):
-            edge(k, banks[k - 3])
+        gather(8, "S", slice(T // 2, T))
+        for k in (4, 5):
+            edge(k, banks[k - 4])
+        free = [0, 1, 2] + banks[2:] + [3] + banks[:2] + [0, 1]
         for k in (6, 7, 8):
-            gather(k, "plain" if k < 8 else "add")
-            edge(k)
-        edge(12)
+            gather(k, "plain", slice(0, T if k < 8 else T // 2))
+            edge(k, free.pop(0))
+        edge(12, free.pop(0))
         for k in (9, 13, 10, 14, 15, 11):
             gather(k, "add")
-            edge(k)
-        held([P, 2 * H], BF16, "w3_dealt1", SLOT * 13)
+            edge(k, free.pop(0))
+        held([P, 2 * H], BF16, "w3_dealt1", SLOT * 16)
         cast3(2, "S", "p m j t")
         cast3(3, "S", "p m j t")
         running(1, 0, 2)

from contextlib import ExitStack

import concourse.mybir as mybir
from concourse.masks import make_identity

F32 = mybir.dt.float32
BF16 = mybir.dt.bfloat16
I32 = mybir.dt.int32
U32 = mybir.dt.uint32
U16 = mybir.dt.uint16
U8 = mybir.dt.uint8
FP8X4 = mybir.dt.float8_e4m3fn_x4
SILU = mybir.ActivationFunctionType.Silu
COPY = mybir.ActivationFunctionType.Copy
MAX = mybir.AluOpType.max
ADD = mybir.AluOpType.add
MULT = mybir.AluOpType.mult

P = 128
T = 512
H = 512
D = 4
WINDOW = 704
FLOPS = 3 * 2 * 512 * 512 * 512
U_BANKS, MM_BANKS = 4, 4
SLOT = 4 * T
STAGE = 17 * SLOT


def tile_picked_wedgecv_silu_lo_kernel(
    tc, x_words, x_scales, w1, w2, w3, pos1, pos2, pos3, pos4, out_0, out_1, out_2
):
    nc = tc.nc
    with ExitStack() as ctx:
        keep = ctx.enter_context(tc.tile_pool(name="keep", bufs=1))
        work = ctx.enter_context(tc.tile_pool(name="work", bufs=1))
        ring = ctx.enter_context(tc.tile_pool(name="ring", bufs=1))
        psum = ctx.enter_context(tc.psum_pool(name="psum", bufs=1))
        tiles = {}

        def held(shape, dtype, name, tag=None):
            if isinstance(tag, int):
                tiles[name] = ring.tile(shape, dtype, name=name, tag=name, bufs=1, align_bytes=64, offset=tag)
            else:
                tiles[name] = work.tile(shape, dtype, name=name, tag=tag or name, bufs=1, align_bytes=64)
            return tiles[name]

        def copy(e, out, in_):
            if e == "S":
                nc.scalar.copy(out=out, in_=in_)
            elif e == "G":
                nc.gpsimd.tensor_scalar(out=out, in0=in_, scalar1=1.0, scalar2=0.0, op0=MULT, op1=ADD)
            else:
                nc.vector.tensor_copy(out=out, in_=in_)

        x_codes = held([P, T], U32, "x_codes")
        x_plane = held([P, T], U8, "x_plane")
        nc.vector.memset(x_plane[:].bitcast(I32), 0)
        wv = {k: w.rearrange("(p j) c -> p j c", j=4) for k, w in ((1, w1), (2, w2), (3, w3))}
        lists = [keep.tile([P, T // 16], U16, name="list%d" % d) for d in range(D)]
        pos = (pos1, pos2, pos3, pos4)
        xs = x_scales[0].bitcast(I32)
        raw = {}

        def load_w(which, t0, t1, over=None):
            if over:
                wide_tile = held([P, T * max(len(over), t1 - t0)], F32, "raw%d_%d" % (which, t0), SLOT * over[0])
                r = wide_tile[:, 0 : T * (t1 - t0)].rearrange("p (j c) -> p j c", j=4)
            else:
                r = held([P, 4, P * (t1 - t0)], F32, "raw%d_%d" % (which, t0))[:]
            nc.sync.dma_start(out=r, in_=wv[which][:, :, P * t0 : P * t1])
            for t in range(t0, t1):
                raw[which, t] = r[:, :, P * (t - t0) : P * (t - t0 + 1)]

        def load_x():
            nc.sync.dma_start(out=x_codes[:].bitcast(I32), in_=x_words[0].rearrange("p c r -> p (c r)").bitcast(I32))

        def load_scales(*queues):
            for q in range(4):
                queues[q * len(queues) // 4].dma_start(out=x_plane[32 * q : 32 * q + 4, :].bitcast(I32), in_=xs[4 * q : 4 * q + 4, :])

        def load_list(d):
            nc.sync.dma_start(lists[d][:], pos[d])

        load_w(2, 0, 1)
        load_x()
        load_scales(nc.sync)
        load_w(1, 0, 1)
        load_list(0)
        load_w(2, 1, 2)
        load_list(1)
        load_w(1, 1, 2, (2, 3))
        load_list(2)
        load_w(2, 2, 4, (4,))
        load_list(3)
        load_w(1, 2, 4, (6, 7))
        load_w(3, 0, 4)

        zero = held([P, 1], F32, "zero")
        warm = held([P, 1], F32, "warm")
        nc.vector.memset(zero[:], 0.0)
        nc.scalar.activation(out=warm[:], in_=zero[:], func=SILU)
        ident = held([P, P], F32, "ident")
        make_identity(nc, ident[:])
        e_sb = [held([P, WINDOW], F32, "e%d" % t) for t in range(4)]
        for t in range(4):
            nc.gpsimd.memset(e_sb[t][:, T:WINDOW], 0.0)
        y_sb = {t: held([P, T], F32, "y%d" % t) for t in range(4)}
        s = [held([P, 4 * H], BF16, "s%d" % d)[:].rearrange("p (b h c) -> p b h c", b=4, h=2) for d in range(D)]
        o_codes = held([P, T], U32, "o_codes")
        o_plane = held([P, T], U8, "o_plane")
        o0v = out_0.rearrange("(p t) v -> p t v", t=4)
        o1v = out_1[0].rearrange("p c r -> p (c r)").bitcast(I32)
        o2v = out_2[0].bitcast(I32)

        products = []
        top = {}
        coded = {}
        wide = {}
        plain = {}
        sums = {}
        place = {}

        def bank(shape, k):
            return psum.tile(shape, F32, name="bank", tag="bank%d" % k, bufs=1)

        def quant(g, n, name, tag=None):
            codes = held([P, n], U32, name + "_codes", tag)
            plane = held([P, n], U8, name + "_plane")
            nc.vector.quantize_mx(out=codes[:].bitcast(FP8X4), scales=plane[:], in_=g)

        def stage(group, tag, room=0):
            held([P, 4 * P * max(len(group), room)], BF16, "c%d_%d" % group[0], tag)

        def cast(group, e, keys):
            g = tiles["c%d_%d" % group[0]]
            order = "p c i j" if e == "G" else "p c j i"
            for key in keys:
                n = group.index(key)
                copy(
                    e,
                    g[:, 4 * P * n : 4 * P * (n + 1)].rearrange("p (c i j) -> " + order, i=4, j=4),
                    raw[key].rearrange("p j (c i) -> " + order, i=4),
                )

        def squeeze_w(group, tag=None):
            name = "w%d_%d" % group[0]
            quant(tiles["c%d_%d" % group[0]][:, 0 : 4 * P * len(group)], P * len(group), name, tag)
            for n, key in enumerate(group):
                cols = slice(P * n, P * (n + 1))
                coded[key] = (tiles[name + "_codes"][:, cols], tiles[name + "_plane"][:, cols])

        def quant3(tag):
            codes = held([P, H], U32, "w3_codes", tag)
            plane = held([P, H], U8, "w3_plane")
            for pair in range(2):
                cols = slice(2 * P * pair, 2 * P * (pair + 1))
                nc.vector.quantize_mx(out=codes[:, cols].bitcast(FP8X4), scales=plane[:, cols], in_=tiles["w3_dealt%d" % pair][:])

        def cast3(a, e, order):
            pair, rows = a // 2, slice(64 * (a % 2), 64 * (a % 2 + 1))
            copy(
                e,
                tiles["w3_dealt%d" % pair][:].rearrange("p (t m j) -> " + order, t=2, j=4)[:, rows],
                tiles["raw3_0"][:].rearrange("p j (m t) -> p m j t", t=4)[:, rows, :, 2 * pair : 2 * pair + 2].rearrange("p m j t -> " + order),
            )

        def product(which, t, es):
            dest = (e_sb if which == 2 else y_sb)[t]
            n = T // len(es)
            for a, e in enumerate(es):
                cols = slice(n * a, n * (a + 1))
                acc = bank([P, n], U_BANKS + len(products) % MM_BANKS)
                products.append(t)
                nc.tensor.matmul_mx(
                    out=acc[:],
                    lhsT=coded[which, t][0].bitcast(FP8X4),
                    lhsT_scale=coded[which, t][1],
                    rhs=x_codes[:, cols].bitcast(FP8X4),
                    rhs_scale=x_plane[:, cols],
                    start=True,
                    stop=True,
                )
                copy(e, dest[:, cols], acc[:])
            return U_BANKS + (len(products) - 1) % MM_BANKS

        def gather(k, how, cols=slice(0, T)):
            t, d = divmod(k, D)
            if "g%d" % k not in tiles:
                held([P, T], F32, "g%d" % k, SLOT * {5: 16, 11: 16}.get(k, k))
            g = tiles["g%d" % k]
            picked = e_sb[t][:].indirect(lists[d][:, cols.start // 16 : cols.stop // 16])
            if how == "S":
                nc.scalar.activation(out=g[:, cols], in_=picked, func=COPY)
            elif how == "plain":
                nc.vector.tensor_copy(out=g[:, cols], in_=picked)
            else:
                nc.vector.tensor_tensor(out=g[:], in0=picked, in1=y_sb[t][:], op=ADD)
            plain[k] = how != "add"

        def move(u, source, start, stop):
            for b in range(4):
                nc.tensor.matmul(
                    u[:, P * b : P * (b + 1)], lhsT=source[:, P * b : P * (b + 1)], rhs=ident[:], is_transpose=True,
                    start=(start and b == 0), stop=(stop and b == 3),
                )

        def begin(k, after=None):
            place[k] = len(place) % U_BANKS if after is None else after
            sums[k] = bank([P, T], place[k])
            move(sums[k], tiles["g%d" % k], True, not plain[k])

        def edge(k, after=None):
            t, d = divmod(k, D)
            if k not in sums:
                begin(k, after)
            u = sums[k]
            if plain[k]:
                move(u, y_sb[t], False, True)
            nc.scalar.activation(
                out=s[d][:, :, :, 64 * t : 64 * (t + 1)].rearrange("p b h (q i) -> p h b q i", i=2),
                in_=u[:].rearrange("p (b q h i) -> p h b q i", h=2, q=32, i=2),
                func=SILU,
            )

        def running(d, b0, nb, tag=None):
            dest = held([P, nb * H], BF16, "m%d_%d" % (d, b0), tag)
            for b in range(b0, b0 + nb):
                top[d, b] = dest[:, H * (b - b0) : H * (b - b0 + 1)]
            span = slice(b0, b0 + nb)
            first = s[0][:, span].rearrange("p b h c -> p (b h c)") if d == 1 else wide[d - 1, b0, nb]
            nc.vector.tensor_tensor(out=dest[:], in0=first, in1=s[d][:, span].rearrange("p b h c -> p (b h c)"), op=MAX)
            for c0 in range(nb):
                for cn in range(1, nb - c0 + 1):
                    wide[d, b0 + c0, cn] = dest[:, H * c0 : H * (c0 + cn)]

        def turn(b, e, k):
            zp = bank([P, 2, P], k)
            for h in range(2):
                nc.tensor.transpose(zp[:, h, :], top[D - 1, b][:, 2 * P * h : 2 * P * (h + 1)].bitcast(F32), ident[:])
            zq = held([P, P * 4], BF16, "zq%d" % b)
            copy(e, zq[:].bitcast(F32).rearrange("p (v h) -> p v h", h=2), zp[:].rearrange("p h v -> p v h"))

        def squeeze(b):
            quant(tiles["zq%d" % b][:], P, "z%d" % b)

        def project(b, es, ks, direct=False, parts=(slice(0, P),)):
            o_sb = held([P, 4, P], F32, "o%d" % b)
            ob = held([P, 4 * P], BF16, "ob%d" % b)
            per = 4 // len(es)
            for a, e in enumerate(es):
                acc = bank([P, per, P], ks[a])
                for t in range(per * a, per * (a + 1)):
                    nc.tensor.matmul_mx(
                        out=acc[:, t - per * a, :],
                        lhsT=tiles["w3_codes"][:, P * t : P * (t + 1)].bitcast(FP8X4),
                        lhsT_scale=tiles["w3_plane"][:, P * t : P * (t + 1)],
                        rhs=tiles["z%d_codes" % b][:].bitcast(FP8X4),
                        rhs_scale=tiles["z%d_plane" % b][:],
                        start=True,
                        stop=True,
                    )
                if direct:
                    copy("V", ob[:].rearrange("p (v t) -> p v t", t=4), acc[:].rearrange("p t v -> p v t"))
                rows = slice(per * a, per * (a + 1))
                for cols in parts:
                    copy(e, o_sb[:, rows, cols], acc[:, :, cols])
                nc.sync.dma_start(out=o0v[:, rows, P * b : P * (b + 1)], in_=o_sb[:, rows, :])

        def rounded(b, e, parts):
            for cols in parts:
                copy(
                    e,
                    tiles["ob%d" % b][:, 4 * cols.start : 4 * cols.stop].rearrange("p (v i t) -> p v t i", i=4, t=4),
                    tiles["o%d" % b][:, :, cols].rearrange("p t (v i) -> p v t i", i=4),
                )

        def planes(b):
            cols = slice(P * b, P * (b + 1))
            nc.vector.quantize_mx(out=o_codes[:, cols].bitcast(FP8X4), scales=o_plane[:, cols], in_=tiles["ob%d" % b][:])

        def words(b0, nb):
            cols = slice(P * b0, P * (b0 + nb))
            nc.sync.dma_start(out=o1v[:, cols], in_=o_codes[:, cols].bitcast(I32))

        second, third, fourth = [[(2, t), (1, t)] for t in (1, 2, 3)]
        for key, es, tag in (((2, 0), "SS", STAGE), ((1, 0), "S", None)):
            stage([key], "first")
            cast([key], "V", [key])
            squeeze_w([key], tag)
            product(*key, es)
            if tag:
                stage(second, tag, 4)
            cast(second, "S", [(key[0], 1)])
        gather(0, "plain")
        edge(0)
        gather(1, "plain")
        squeeze_w(second)
        stage(third, STAGE)
        stage(fourth, STAGE + SLOT)
        cast(fourth, "G", [(2, 3)])
        cast(third, "G", [(1, 2)])
        cast(fourth, "G", [(1, 3)])
        cast(third, "S", [(2, 2)])
        for key in second:
            product(*key, "S")
        gather(4, "S")
        edge(1)
        gather(2, "plain")
        edge(2)
        gather(3, "plain")
        edge(3)
        gather(5, "plain")
        squeeze_w(third)
        squeeze_w(fourth)
        held([P, 2 * H], BF16, "w3_dealt0", STAGE)
        cast3(0, "G", "p m t j")
        cast3(1, "G", "p m t j")
        banks = [product(*key, "S") for key in third + fourth]
        gather(12, "S")
        gather(8, "S", slice(T // 2, T))
        for k in (4, 5):
            edge(k, banks[k - 4])
        free = [0, 1, 2] + banks[2:] + [3] + banks[:2] + [0, 1]
        for k in (6, 7, 8):
            gather(k, "plain", slice(0, T if k < 8 else T // 2))
            edge(k, free.pop(0))
        edge(12, free.pop(0))
        for k in (9, 13, 10, 14, 15, 11):
            gather(k, "add")
            edge(k, free.pop(0))
        held([P, 2 * H], BF16, "w3_dealt1", SLOT * 16)
        cast3(2, "S", "p m j t")
        cast3(3, "S", "p m j t")
        running(1, 0, 2)
        running(1, 2, 2)
        running(2, 0, 2)
        running(2, 2, 2)
        for b in range(4):
            running(3, b, 1)
        quant3("m2_0")
        for b in range(4):
            turn(b, "S", 4 + b)
            squeeze(b)
        whole, halves = (slice(0, P),), (slice(0, P // 2), slice(P // 2, P))
        project(0, "SS", [0, 4])
        for b in range(1, 4):
            project(b, "S", [b], False, halves if b == 3 else whole)
        for b in range(4):
            rounded(b, "V", halves if b == 3 else whole)
            planes(b)
            if b % 2:
                words(b - 1, 2)
        for q in range(4):
            (nc.scalar if q % 2 else nc.sync).dma_start(
                out=o2v[4 * q : 4 * q + 4, :], in_=o_plane[32 * q : 32 * q + 4, :].bitcast(I32)
            )
